import numpy as np, ml_dtypes
CORES = [24,25,26,27,28,29,30,31]
N = 8
BF = ml_dtypes.bfloat16
def gentries(a):
    return np.ascontiguousarray(a.reshape(8, 16, -1).transpose(0, 2, 1)).reshape(8, -1)
def gtable(e):
    e = np.asarray(e); return np.ascontiguousarray(e.reshape(8, -1, 16).transpose(0, 2, 1)).reshape(128, -1).astype(np.int32)
R, H, LO, UP, SW = 384, 32, 3, 6, 4
S, M, T = LO + 1 + UP, N * R, R + (N - 1) * H
def byrank(v):
    return np.ascontiguousarray(v.reshape(8, -1, R, N).transpose(3, 0, 1, 2)).reshape(N, 8, -1)
def ships(rng, rows):
    return np.argsort(rng.random((N, 8, N - 1, rows)), axis=-1)[..., :H]
def users(rng, low):
    u = np.full((8, M), -1, np.int64)
    for g in range(8):
        for t in rng.permutation(LO):
            o = rng.permutation(M); l = low[g, t, o]; ok = l >= 0; u[g, l[ok]] = o[ok]
    return u
def grow(rng, ship, far, drop=0.05, sweep=False):
    G = np.arange(8)[:, None]; i = np.arange(M); q = i % N; n = i // N; K = (N - 1) * H
    low = np.empty((8, LO, M), np.int64); spot = np.empty((8, LO, M), np.int64); up = np.empty((8, UP, M), np.int64)
    for t in range(LO):
        e = rng.integers(0, K, (8, M))
        if sweep: e = np.where(n >= R // 2, ((n - R // 2) * LO + t) % K, e)
        b = e // H; p = b + (b >= q); k = ship[p, G, q - (q > p), e % H] * N + p
        take = (rng.random((8, M)) < far) & (k < i); own = (rng.random((8, M)) * n).astype(np.int64)
        c = np.where(take, k, own * N + q); none = (~take & (n == 0)) | (rng.random((8, M)) < drop)
        for s in range(t): none |= c == low[:, s]
        low[:, t] = np.where(none, -1 - t, c); spot[:, t] = np.where(none, rng.integers(0, T, (8, M)), np.where(take, R + e, own))
    u = users(rng, low); cand = []
    for x in (u, users(rng, low)):
        v = np.maximum(x, 0); l = low[G, rng.integers(0, LO, (8, M)), v]
        cand += [x, np.where((x >= 0) & (l > i), l, -1), np.where(x >= 0, u[G, v], -1)]
    cand = np.stack(cand); turn = rng.integers(0, UP, (8, M))
    for w in range(UP):
        c = cand[(w + turn) % UP, G, i]; other = i + 1 + (rng.random((8, M)) * (M - 1 - i)).astype(np.int64)
        good = (c > i) & (rng.random((8, M)) < 0.85)
        for s in range(w): good &= c != up[:, s]
        c = np.where(good, c, other); none = (c >= M) | (rng.random((8, M)) < 0.04)
        for s in range(w): none |= c == up[:, s]
        up[:, w] = np.where(none, M + w, c)
    return low, spot, up
def fill(rng, ship, low, spot, up):
    c = np.concatenate([low, np.broadcast_to(np.arange(M), (8, 1, M)), up], 1); real = byrank((c >= 0) & (c < M)).reshape(N, 8, 1, S, R)
    v = (0.03 + 0.09 * rng.random((N, 8, 16, S, R))) * (2 * rng.integers(0, 2, (N, 8, 16, S, R)) - 1)
    v = np.where(real, v, 0.0); v[:, :, :, LO] = 0.75 + 0.75 * rng.random((N, 8, 16, R))
    return {"val": v.reshape(N, 128, S * R).astype(BF), "col": byrank(c).astype(np.int32), "spot": np.stack([gtable(x) for x in byrank(spot)]), "ship": np.stack([gtable(x.reshape(8, -1)) for x in ship])}
def setup_inputs(rng):
    ship = ships(rng, R); return fill(rng, ship, *grow(rng, ship, 0.8))
def setup_inputs_halo(rng):
    ship = ships(rng, R // 2); return fill(rng, ship, *grow(rng, ship, 1.0, 0.0, True))
def setup_inputs_hub(rng):
    ship = rng.integers(0, 3, (N, 8, N - 1, H)); return fill(rng, ship, *grow(rng, ship, 0.95))
def setup_inputs_thin(rng):
    ship = ships(rng, R); low, spot, up = grow(rng, ship, 0.8)
    gone = rng.random((8, 1, M)) < rng.permutation(np.array([1.0, 1.0, 0.95, 0.8, 0.5, 0.5, 0.1, 0.0]))[:, None, None]
    gone = gone | (np.arange(M) % N == rng.integers(0, N))
    low = np.where(gone, -1 - np.arange(LO)[:, None], low); up = np.where(gone, M + np.arange(UP)[:, None], up)
    return fill(rng, ship, low, spot, up)
def setup_inputs_band(rng):
    ship = ships(rng, R); low, spot, up = grow(rng, ship, 0.8); n = np.arange(M) // N; q = np.arange(M) % N
    for g in range(6):
        for t in range(LO):
            b = n - (t + 1) * (g + 1); low[g, t] = np.where(b >= 0, b * N + q, -1 - t); spot[g, t] = np.where(b >= 0, b, 0)
        for w in range(UP):
            b = n + (w + 1) * (g + 1); up[g, w] = np.where(b < R, b * N + q, M + w)
    d = fill(rng, ship, low, spot, up); v = np.sign(d["val"].astype(np.float32)).reshape(N, 8, 16, S, R) * (0.125 - rng.integers(0, 4, (N, 8, 16, S, R)) * 2.0 ** -11)
    v[:, :, :, LO] = rng.choice(np.array([0.75, 0.75390625, 1.4921875, 1.5]), (N, 8, 16, R)); d["val"] = v.reshape(N, 128, S * R).astype(np.float32).astype(BF); return d
def setup_inputs_spread(rng):
    d = setup_inputs(rng); k = np.exp2(rng.integers(-6, 1, (N, 8, 1, S, R))) * (rng.random((N, 8, 1, S, R)) > 0.0625); k[:, :, :, LO] = 1
    d["val"] = (d["val"].astype(np.float32).reshape(N, 8, 16, S, R) * k).reshape(N, 128, S * R).astype(BF); return d
def check_inputs(d):
    bad = []; i = np.arange(R)[None] * N + np.arange(N)[:, None]; row = i[:, None, None]
    c = d["col"].astype(np.int64).reshape(N, 8, S, R); lo, up = c[:, :, :LO], c[:, :, LO + 1:]
    elo = lo == -1 - np.arange(LO)[:, None]; eup = up == M + np.arange(UP)[:, None]
    if not (c[:, :, LO] == i[:, None]).all(): bad.append("the diagonal's column is the row's number")
    if not (elo | ((lo >= 0) & (lo < row))).all(): bad.append("lower columns are below the row's number, or the slot is empty")
    if not (eup | ((up > row) & (up < M))).all(): bad.append("upper columns are above the row's number, or the slot is empty")
    s = np.sort(c, axis=2)
    if (s[:, :, 1:] == s[:, :, :-1]).any(): bad.append("the columns of a row differ")
    v = d["val"].astype(np.float32).reshape(N, 8, 16, S, R); e = np.concatenate([elo, np.zeros((N, 8, 1, R), bool), eup], 2)[:, :, None]
    if not ((v[:, :, :, LO] >= 0.75) & (v[:, :, :, LO] <= 1.5)).all(): bad.append("diagonals lie from 0.75 to 1.5")
    if not (np.abs(np.delete(v, LO, 3)) <= 0.125).all(): bad.append("other values are at most 0.125 in size")
    if not ((v == 0) | ~e).all(): bad.append("empty slots have the value 0")
    sh = np.stack([gentries(x) for x in d["ship"]]).astype(np.int64).reshape(N, 8, N - 1, H); sp = np.stack([gentries(x) for x in d["spot"]]).astype(np.int64)
    if not ((sh >= 0) & (sh < R)).all(): bad.append("ship names local rows")
    if not ((sp >= 0) & (sp < T)).all(): bad.append("spot holds places")
    for q in range(N):
        tab = np.concatenate([np.broadcast_to(i[q], (8, R))] + [sh[p][:, q - (q > p)] * N + p for p in range(N) if p != q], 1)
        k = np.take_along_axis(tab, np.clip(sp[q], 0, T - 1), 1).reshape(8, LO, R)
        if not ((k == lo[q]) | elo[q]).all(): bad.append("the row at a lower slot's place is its column"); break
    return bad
def reference(val, col, spot, ship):
    c = col.astype(np.int64).reshape(N, 8, S, R).transpose(1, 2, 3, 0).reshape(8, S, M)
    a = val.astype(np.float64).reshape(N, 8, 16, S, R).transpose(1, 2, 3, 4, 0).reshape(8, 16, S, M)
    y = np.empty((8, 16, S, M)); z = np.empty((8, 16, M))
    for g in range(8):
        k = np.maximum(c[g, :LO], 0)
        at = np.full((S, LO, M), UP * M, np.int64)
        for w in range(UP): at = np.where(c[g, LO + 1 + w][k][None] == c[g][:, None], w * M + k[None], at)
        x = a[g]; r = np.ones((16, M))
        for sweep in range(SW):
            u = np.concatenate([x[:, LO + 1:].reshape(16, UP * M), np.zeros((16, 1))], 1); d = np.array(a[g])
            for t in range(LO): d -= x[:, t][:, None] * u[:, at[:, t]]
            for t in range(LO): d[:, t] *= r[:, k[t]]
            r = r * (2 - x[:, LO] * r); x = d
        y[g] = x; z[g] = r
    y = y.reshape(8, 16, S, R, N).transpose(4, 0, 1, 2, 3).reshape(N, 128, S * R); z = z.reshape(8, 16, R, N).transpose(3, 0, 1, 2).reshape(N, 128, R)
    return {"y": y.astype(np.float32), "inv": z.astype(np.float32)}

@@ -1,0 +1,453 @@
+from concourse.bass import DstId, RemoteDMATransfer
+from concourse.mybir import AluOpType as OP, ActivationFunctionType as AF
+
+NR, R, H, PL = 8, 384, 32, 608
+K = (NR - 1) * H
+B = 3
+NB = 6 // B
+PAD, BIG = 16, 4096
+TL = PAD + 6 * PL
+HD, COFF = "float16", 1536
+VG = (0, 1, 2, 3, 4, 5, 6, 7, 8)
+NPE = (2, 2, 2, 2, 2, 2, 2)
+NT = (3, 3, 3, 3, 3, 3, 3, 2, 1)
+
+SCRATCH = {
+    "shipi": ("sbuf", [128, 16], "int32"), "spoti": ("sbuf", [128, 72], "int32"),
+    "colw": ("sbuf", [128, PL], "int32"), "csend": ("sbuf", [128, K], "int32"),
+    "shipu": ("sbuf", [128, 16], "uint16"), "shipo": ("sbuf", [128, 14 * 6 + 12], "uint16"),
+    "spo": ("sbuf", [128, 72], "uint16"), "spu": ("sbuf", [128, 72], "uint16"),
+    "pru": ("sbuf", [128, 72], "uint16"), "ivu": ("sbuf", [128, 72], "uint16"),
+    "off": ("sbuf", [128, 648], "uint16"),
+    "vb": ("sbuf", [128, 10 * R], "bfloat16"), "asr": ("sbuf", [128, 3 * R], "bfloat16"),
+    "colh": ("sbuf", [128, R], HD), "ot": ("sbuf", [128, 3 * R], HD),
+    "cg": ("sbuf", [128, 3 * R], HD), "ct": ("sbuf", [128, 3 * R], HD),
+    "ones": ("sbuf", [128, 128], "bfloat16"), "sel": ("sbuf", [128, 512], "bfloat16"),
+    "idn": ("sbuf", [128, 128], "bfloat16"), "negi": ("sbuf", [128, 128], "float32"),
+    "wm": ("sbuf", [128, 128 * 6], "bfloat16"),
+    "o3": ("sbuf", [128, 648], "float32"), "kk": ("sbuf", [128, 144], "float32"),
+    "net": ("sbuf", [128, 144], "float32"), "srt": ("sbuf", [128, 144], "float32"),
+    "pay": ("sbuf", [128, 72], "float32"), "tmp": ("sbuf", [128, 72], "float32"),
+    "ki": ("sbuf", [128, 72], "int32"), "kj": ("sbuf", [128, 72], "int32"), "kt": ("sbuf", [128, 72], "int32"),
+    "nsp": ("sbuf", [128, 216], "float32"), "n3": ("sbuf", [128, 72], "float32"), "n3i": ("sbuf", [128, 72], "int32"),
+    "pi": ("sbuf", [128, 4], "int32"), "pj": ("sbuf", [128, 4], "int32"), "pf": ("sbuf", [128, 4], "float32"),
+    "ta": ("sbuf", [128, 72], "float32"), "tb": ("sbuf", [128, 72], "float32"),
+    "ext": ("sbuf", [128, 120], "float32"), "ga": ("sbuf", [128, 72], "float32"), "gb": ("sbuf", [128, 72], "float32"),
+    "eq": ("sbuf", [128, 54 * 72], "bfloat16"),
+    "u0": ("sbuf", [128, TL], "bfloat16"), "u1": ("sbuf", [128, TL], "float32"),
+    "u2": ("sbuf", [128, TL], "float32"), "u3": ("sbuf", [128, TL], "float32"),
+    "s0": ("sbuf", [128, 6 * K], "bfloat16"), "s1": ("sbuf", [128, 6 * K], "float32"),
+    "s2": ("sbuf", [128, 6 * K], "float32"), "s3": ("sbuf", [128, 6 * K], "float32"),
+    "rt1": ("sbuf", [128, PL], "float32"), "rt2": ("sbuf", [128, PL], "float32"),
+    "rt3": ("sbuf", [128, PL], "float32"), "rt4": ("sbuf", [128, R], "float32"),
+    "rs": ("sbuf", [128, 3 * K], "float32"),
+    "gg": ("sbuf", [128, 8 * 3 * R + R], "float32"), "pp": ("sbuf", [128, 8 * 3 * R + R], "float32"),
+    "x0": ("sbuf", [128, R], "float32"), "rr": ("sbuf", [128, 3 * R], "float32"),
+    "d4": ("sbuf", [128, 3 * R], "float32"), "yb": ("sbuf", [128, 10 * R], "float32"),
+    "ps": ("psum", [128, 4096], "float32"),
+}
+SEMAPHORES = ["ev", "es", "ep", "eg", "lship", "lspot", "lcol", "lu0", "lu1", "llow", "st", "sent", "csent",
+              "acol", "au0", "au1", "au2", "au3", "ar1", "ar2", "ar3"]
+
+
+def _clash(a, b, any_use):
+    for n, lo, hi, st in a:
+        for m, l2, h2, s2 in b:
+            if n == m and lo < h2 and l2 < hi and (n == "ps" or not any_use):
+                if st == 1 or st != s2 or (lo - l2) % st == 0:
+                    return True
+    return False
+
+
+def _emit(g, T, ops, tail):
+    q = {"v": g.vector, "s": g.scalar, "p": g.tensor, "g": g, "y": g.sync}
+    known = {e: {} for e in q}
+    seq = {e: 0 for e in q}
+    need = {e: set() for e in q}
+    for i, o in enumerate(ops):
+        e = o["e"]
+        if e is None:
+            o["clock"] = {o["tok"][0]: o["tok"][1]}
+            continue
+        waits = []
+        for d in range(i - 1, -1, -1):
+            p = ops[d]
+            key, val = p["tok"]
+            if known[e].get(key, 0) >= val:
+                continue
+            if e == "p" and key == "p":
+                continue
+            if o["tok"] is not None and key == o["tok"][0]:
+                continue
+            hit = _clash(o["r"], p["w"], False) or _clash(o["w"], p["w"], False) or _clash(o["w"], p["r"], False)
+            if not hit and p["e"] != e:
+                hit = _clash(o["r"], p["r"], True)
+            if hit or d in o["after"]:
+                waits.append((key, val))
+                for k2, v2 in p["clock"].items():
+                    known[e][k2] = max(known[e].get(k2, 0), v2)
+        o["waits"] = waits
+        for key, val in waits:
+            if key in need:
+                need[key].add(val)
+        if o["tok"] is None:
+            seq[e] += 1
+            o["tok"] = (e, seq[e])
+        o["clock"] = dict(known[e])
+        o["clock"][o["tok"][0]] = max(o["tok"][1], o["clock"].get(o["tok"][0], 0))
+    count = {e: {v: j + 1 for j, v in enumerate(sorted(need[e]))} for e in need}
+    for o in ops:
+        e = o["e"]
+        if e is None:
+            continue
+        for key, val in o["waits"]:
+            if key in count:
+                q[e].wait_ge(T.sem["e" + key], count[key][val])
+            else:
+                q[e].wait_ge(T.sem[key], val)
+        ins = o["f"]()
+        key, val = o["tok"]
+        if key in count:
+            if val in count[key]:
+                ins.then_inc(T.sem["e" + key], 1)
+        elif o["inc"]:
+            ins.then_inc(T.sem[key], 16)
+    for e, key, val in tail:
+        q[e].wait_ge(T.sem[key], val)
+
+
+def rank_program(g, core, T, topo):
+    rank = T.rank_of(core)
+    if rank is None:
+        return
+    ops = []
+
+    def A(n, lo, hi, st=1):
+        ap = T[n][:, lo:hi:st] if st > 1 else T[n][:, lo:hi]
+        if n == "ps":
+            lo, hi, st = lo // 512 * 512, (hi + 511) // 512 * 512, 1
+        return (ap, [(n, lo, hi, st)])
+
+    def IND(win, off):
+        return (win[0].indirect(off[0]), win[1] + off[1])
+
+    def op(e, f, r, w, tok=None, inc=False, after=()):
+        ops.append({"e": e, "f": f, "r": [x for a in r for x in a[1]], "w": [x for a in w for x in a[1]],
+                    "tok": tok, "inc": inc, "after": set(after)})
+        return len(ops) - 1
+
+    def tt(o, a, b, alu):
+        op("v", lambda: g.vector.tensor_tensor(o[0], a[0], b[0], alu), [a, b], [o])
+
+    def ts(o, a, s1, o0, s2=None, o1=None):
+        col = isinstance(s1, tuple)
+        x1 = s1[0] if col else s1
+        if o1 is None:
+            op("v", lambda: g.vector.tensor_scalar(o[0], a[0], x1, None, o0), [a] + ([s1] if col else []), [o])
+        else:
+            op("v", lambda: g.vector.tensor_scalar(o[0], a[0], x1, s2, o0, o1), [a] + ([s1] if col else []), [o])
+
+    def cp(o, a):
+        op("v", lambda: g.vector.tensor_copy(o[0], a[0]), [a], [o])
+
+    def ms(o, c):
+        op("v", lambda: g.vector.memset(o[0], c), [], [o])
+
+    def tr(o, a):
+        op("v", lambda: g.vector.transpose(o[0], a[0]), [a], [o])
+
+    def sc(o, a, scale=None, bias=None):
+        if scale is None:
+            op("s", lambda: g.scalar.activation(o[0], a[0], AF.Copy), [a], [o])
+        else:
+            op("s", lambda: g.scalar.activation(o[0], a[0], AF.Identity, bias=float(bias), scale=float(scale)), [a], [o])
+
+    def mm(o, l, r, start, stop):
+        op("p", lambda: g.tensor.matmul(o[0], l[0], r[0], start, stop), [l, r], [o])
+
+    def dma(e, o, a, tok, after=()):
+        qq = g.sync if e == "y" else g.scalar
+        op(e, lambda: qq.dma_start(o[0], a[0]), [a], [o], tok=tok, inc=True, after=after)
+
+    peers = [c for c in T.cores if c != core]
+    masks, used = {}, [0, 0]
+    for c in peers:
+        far = 0 if topo.die(c) != topo.die(core) else 1
+        eng = topo.engines(core, c)[far::2][used[far]:used[far] + 2]
+        used[far] += 2
+        masks[c] = (1 << eng[0]) | (1 << eng[1])
+    INC = 2 * len(peers)
+    nsent = [0]
+
+    def send(src, s0, dst, d0, width, sem, local="sent"):
+        trs = []
+        for b, c in enumerate(peers):
+            qr = T.rank_of(c)
+            bb = rank if rank < qr else rank - 1
+            rid, pid, _ = topo.addr(c)
+            trs.append(RemoteDMATransfer(dst_ids=[DstId(rid=rid, pnc=pid)], dma_engine_mask=masks[c],
+                                         remote_sem=T.sem[sem], src=T[src][:, s0 + b * width:s0 + (b + 1) * width],
+                                         dst=T[dst][:, d0 + bb * width:d0 + (bb + 1) * width]))
+        if local == "sent":
+            nsent[0] += INC
+        tok = (local, INC) if local != "sent" else ("sent", 1 << 20)
+        return op("g", lambda: g.remote_dma_fused(trs, local_sem=T.sem[local]), [A(src, s0, s0 + 7 * width)], [], tok=tok)
+
+    def arrive(regs, sem, val):
+        op(None, None, [], regs, tok=(sem, val))
+
+    def swap(o0, src, lane, n):
+        for c2 in range(2):
+            for g2 in range(2):
+                k = 2 * c2 + g2
+                mm(A("ps", o0 + c2, o0 + 2 * n, 2), A("sel", 128 * k, 128 * k + 128),
+                   A(src, 16 * g2 + lane, 32 * n, 32), g2 == 0, g2 == 1)
+
+    base = [PAD + b * PL * B for b in range(NB)]
+
+    ms(A("colw", 0, R), 0)
+    ms(A("ones", 0, 128), 1.0)
+    dma("y", A("shipi", 0, 14), (T.ship[:], []), ("lship", 16))
+    for gi in range(8):
+        dma("y" if gi % 2 == 0 else "s", (T.colw[16 * gi:16 * gi + 10, 0:R], [("colw", 0, R, 1)]),
+            (T.col[gi:gi + 1, :], []), ("lcol", 128))
+    dma("s", A("spoti", 0, 72), (T.spot[:], []), ("lspot", 16))
+    dma("y", A("vb", 4 * R, 7 * R), (T.val[:, 4 * R:7 * R], []), ("lu0", 16))
+    dma("s", A("vb", 7 * R, 10 * R), (T.val[:, 7 * R:10 * R], []), ("lu1", 16))
+    for c2 in range(2):
+        for g2 in range(2):
+            def f(c2=c2, g2=g2):
+                k = 2 * c2 + g2
+                return g.affine_select(T.sel[:, 128 * k:128 * k + 128], T.ones[:, 0:128],
+                                       [[-32, 4], [1000, 2], [-1, 16]], OP.is_equal, 0.0, -16 * c2 - 1000 * g2, 1)
+            op("g", f, [A("ones", 0, 128)], [A("sel", 128 * (2 * c2 + g2), 128 * (2 * c2 + g2) + 128)])
+    for n in ("u0", "u1", "u2", "u3"):
+        ms(A(n, 0, PAD), 0.0)
+    ms(A("o3", 504, 648), 0.0)
+    cp(A("shipu", 0, 14), A("shipi", 0, 14))
+    cp(A("csend", 0, K), IND(A("colw", 0, R), A("shipu", 0, 14)))
+    cs = send("csend", 0, "colw", R, H, "acol", local="csent")
+    arrive([A("colw", R, PL)], "acol", INC)
+    dma("y", A("vb", 0, 4 * R), (T.val[:, 0:4 * R], []), ("llow", 16), after=[cs])
+    op("g", lambda: g.iota(T.n3i[:, 0:72], [[0, 3], [16, 24]], 0, 1), [], [A("n3i", 0, 72)])
+    op("g", lambda: g.iota(T.pi[:, 0:1], [[0, 1]], 0, 1), [], [A("pi", 0, 1)])
+    ts(A("colh", 0, R), A("colw", 0, R), float(-COFF), OP.add)
+    tr(A("ot", 0, R), A("colh", 0, R))
+    for j, lane in enumerate((0, 1, 2, 0, 1)):
+        swap(3 * 512 + 24 * j, "ot", lane, 12)
+    tr(A("ot", R, 2 * R), A("colh", 0, R))
+    tr(A("ot", 2 * R, 3 * R), A("colh", 0, R))
+    for j, lane in enumerate((4, 5, 6, 7, 8, 9, 3)):
+        swap(2 * 512 + 72 * j, "ot", lane, 36)
+    for t in range(3):
+        ts(A("pay", 24 * t, 24 * t + 24), A("spoti", 24 * t, 24 * t + 24), 4.0, OP.mult, float(t), OP.add)
+    tt(A("idn", 0, 128), A("sel", 0, 128), A("sel", 384, 512), OP.add)
+    ts(A("tmp", 0, 72), A("ps", 1536, 1608), float(COFF + 3), OP.add, 4096.0, OP.mult)
+    cp(A("kk", 1, 144, 2), A("ps", 1536, 1608))
+    cp(A("ext", 0, 120), A("ps", 1536, 1656))
+    tt(A("kk", 0, 144, 2), A("tmp", 0, 72), A("pay", 0, 72), OP.add)
+    for w in range(B):
+        ts(A("shipo", 14 * w, 14 * w + 14), A("shipi", 0, 14), float(B), OP.mult, float(w), OP.add)
+    tt(A("net", 0, 48), A("kk", 0, 48), A("kk", 48, 96), OP.min)
+    tt(A("net", 48, 96), A("kk", 0, 48), A("kk", 48, 96), OP.max)
+    cp(A("spo", 0, 72), A("spoti", 0, 72))
+    tt(A("net", 96, 144), A("net", 48, 96), A("kk", 96, 144), OP.min)
+    tt(A("srt", 96, 144), A("net", 48, 96), A("kk", 96, 144), OP.max)
+    tt(A("ga", 0, 72), A("ext", 0, 72), A("ext", 24, 96), OP.is_gt)
+    tt(A("srt", 0, 48), A("net", 0, 48), A("net", 96, 144), OP.min)
+    tt(A("srt", 48, 96), A("net", 0, 48), A("net", 96, 144), OP.max)
+    tt(A("gb", 0, 72), A("ext", 0, 72), A("ext", 48, 120), OP.is_gt)
+    cp(A("ki", 0, 72), A("srt", 0, 144, 2))
+    ts(A("pj", 0, 1), A("pi", 0, 1), 112, OP.bitwise_and)
+    ts(A("kj", 0, 72), A("ki", 0, 72), 2, OP.arith_shift_right, 1023, OP.bitwise_and)
+    ts(A("kt", 0, 72), A("ki", 0, 72), 3, OP.bitwise_and)
+    cp(A("pf", 0, 1), A("pj", 0, 1))
+    cp(A("spu", 0, 72), A("kj", 0, 72))
+    tt(A("ga", 0, 72), A("ga", 0, 72), A("gb", 0, 72), OP.add)
+    ts(A("n3", 0, 72), A("n3i", 0, 72), A("pf", 0, 1), OP.subtract)
+    ts(A("ta", 0, 72), A("kt", 0, 72), float(R), OP.mult)
+    ts(A("gb", 0, 72), A("ga", 0, 72), float(R), OP.mult)
+    for j in range(3):
+        ts(A("nsp", 72 * j, 72 * j + 72), A("kj", 0, 72), float(-B), OP.mult, float(BIG - PAD), OP.add)
+    tt(A("tb", 0, 72), A("ta", 0, 72), A("n3", 0, 72), OP.add)
+    tt(A("ga", 0, 72), A("gb", 0, 72), A("n3", 0, 72), OP.add)
+    cp(A("o3", 504, 528), A("srt", 97, 144, 2))
+    cp(A("o3", 528, 552), A("srt", 97, 144, 2))
+    cp(A("o3", 576, 600), A("srt", 49, 96, 2))
+    cp(A("pru", 0, 72), A("tb", 0, 72))
+    cp(A("ivu", 0, 72), A("ga", 0, 72))
+    sc(A("negi", 0, 128), A("idn", 0, 128), -1.0, 0.0)
+    wts = sorted(set([BIG + b * PL * B for b in range(NB)] + list(range(2, B))))
+    wat = {1: A("idn", 0, 128)}
+    for j, v in enumerate(wts):
+        wat[v] = A("wm", 128 * j, 128 * j + 128)
+        sc(wat[v], A("idn", 0, 128), v, 0.0)
+    for j in range(3):
+        mm(A("ps", (4 + j) * 512, (4 + j) * 512 + 216), A("negi", 0, 128), A("nsp", 0, 216), True, False)
+    for b in range(NB):
+        for w in range(B):
+            s = 4 + b * B + w
+            sc(A("s0", b * B * K + w, (b + 1) * B * K, B), IND(A("vb", s * R, s * R + R), A("shipu", 0, 14)))
+        send("s0", b * B * K, "u0", base[b] + R * B, H * B, "au0")
+    arrive([A("u0", base[b] + R * B, base[b] + PL * B) for b in range(NB)], "au0", INC * NB)
+    sc(A("o3", 0, 504), A("ps", 1024, 1528))
+    for w in range(6):
+        sc(A("u0", base[w // B] + w % B, base[w // B] + R * B, B), A("vb", (4 + w) * R, (5 + w) * R))
+    sc(A("asr", 0, 3 * R), IND(A("vb", 0, 3 * R), A("pru", 0, 72)))
+
+    def xb(k):
+        return (k % 2) * 1024 + 128
+
+    def rship(k):
+        sc(A("rs", (k - 1) * K, k * K), IND(A("rt%d" % k, 0, R), A("shipu", 0, 14)))
+        send("rs", (k - 1) * K, "rt%d" % k, R, H, "ar%d" % k)
+        arrive([A("rt%d" % k, R, PL)], "ar%d" % k, INC)
+
+    for t in range(3):
+        ts(A("cg", t * R, t * R + R), IND(A("colw", 0, PL), A("spu", 24 * t, 24 * t + 24)), float(-COFF), OP.add)
+        if t:
+            tr(A("ct", t * R - R, t * R), A("cg", t * R - R, t * R))
+    tr(A("ct", 2 * R, 3 * R), A("cg", 2 * R, 3 * R))
+    for w in range(5, -1, -1):
+        swap(296 + 72 * w, "ct", 4 + w, 36)
+    e0 = 0
+    for d in range(-5, 9):
+        w0, w1 = max(0, -d), min(5, 8 - d)
+        n = (w1 - w0 + 1) * 72
+        tt(A("eq", e0, e0 + n), A("o3", (d + w0) * 72, (d + w0) * 72 + n), A("ps", 296 + w0 * 72, 296 + w0 * 72 + n),
+           OP.is_equal)
+        if d in (3, 6):
+            j = d // 3 - 1
+            cp(A("off", 216 * j, 216 * j + 216), A("ps", (4 + j) * 512, (4 + j) * 512 + 216))
+        for w in range(w1, w0 - 1, -1):
+            sg = d + w
+            o = A("ps", (4 + sg // 3) * 512 + (sg % 3) * 72, (4 + sg // 3) * 512 + (sg % 3) * 72 + 72)
+            rhs = A("eq", e0 + (w - w0) * 72, e0 + (w - w0) * 72 + 72)
+            if w % B:
+                mm(o, wat[w % B], rhs, False, False)
+            mm(o, wat[BIG + (w // B) * PL * B], rhs, False, w == 0 and sg % 3 == 2)
+        e0 += n
+    cp(A("off", 432, 648), A("ps", 6 * 512, 6 * 512 + 216))
+    for j in range(2):
+        mm(A("ps", xb(1) + j * R, xb(1) + j * R + R), A("idn", 0, 128), A("asr", R + j * R, 2 * R + j * R), True, True)
+    allv = len(VG) == 9
+    X0P = A("ps", 7 * 512, 7 * 512 + R)
+    if not allv:
+        mm(X0P, A("idn", 0, 128), A("asr", 0, R), True, True)
+    nst = [0]
+
+    def store(lo, hi):
+        nst[0] += 16
+        dma("y", (T.y[:, lo:hi], []), A("yb", lo, hi), ("st", 1 << 20))
+
+    def sweep(k):
+        tin = A("u%d" % (k - 1), 0, TL)
+        x0 = A("asr", 0, R) if k <= 2 else A("x0", 0, R)
+        xo, xn = xb(k), xb(k + 1)
+        nb = 4 if allv else 3
+
+        def acc(s):
+            c = (4 + s % nb) * 512 if s < 7 else xn + (8 - s) * R
+            return A("ps", c, c + R)
+
+        def pr(n, s, t0, t1):
+            return A(n, (3 * s + t0) * R, (3 * s + t1) * R)
+
+        def G(s):
+            t0 = 1 if s in VG else 0
+            if t0 < NT[s]:
+                sc(pr("gg", s, t0, NT[s]), IND(tin, A("off", 72 * s + 24 * t0, 72 * s + 24 * NT[s])))
+
+        def P0(s):
+            if s in VG:
+                tt(pr("pp", s, 0, 1), IND(tin, A("off", 72 * s, 72 * s + 24)), x0, OP.mult)
+            else:
+                tt(pr("pp", s, 0, 1), pr("gg", s, 0, 1), X0P, OP.mult)
+
+        def npe(s):
+            return NPE[s] if s < 7 else (NT[s] if k < 4 else NT[s] - 1)
+
+        def PE(s):
+            a = A("vb", (4 + s) * R, (5 + s) * R) if s < 6 else (A("vb", 3 * R, 4 * R) if s == 6 else
+                                                              A("asr", (9 - s) * R, (10 - s) * R))
+            mm(acc(s), A("idn", 0, 128), a, True, npe(s) == 0)
+            for t in range(npe(s)):
+                mm(acc(s), A("negi", 0, 128), pr("pp", s, t, t + 1), False, t == npe(s) - 1)
+
+        def P12(s):
+            if NT[s] > 1:
+                tt(pr("pp", s, 1, NT[s]), pr("gg", s, 1, NT[s]), A("ps", xo, xo + (NT[s] - 1) * R), OP.mult)
+            PE(s)
+
+        def E(s):
+            if s >= 7:
+                out = A("d4", (9 - s) * R, (10 - s) * R)
+            elif k == 4:
+                sl = 4 + s if s < 6 else 3
+                out = A("yb", sl * R, sl * R + R)
+            elif s < 6:
+                out = A("u%d" % k, base[s // B] + s % B, base[s // B] + R * B, B)
+            else:
+                out = acc(s)
+            for t in range(npe(s), NT[s]):
+                tt(out if t == NT[s] - 1 else acc(s), acc(s), pr("pp", s, t, t + 1), OP.subtract)
+            if npe(s) == NT[s] and (s < 6 or k == 4):
+                sc(out, acc(s))
+            if k == 4 and s < 7:
+                store(sl * R, sl * R + R)
+
+        def ship(*ss):
+            for s in ss:
+                b, w = s // B, s % B
+                sc(A("s%d" % k, b * B * K + w, (b + 1) * B * K, B),
+                   IND(A("u%d" % k, base[b], base[b] + R * B), A("shipo", 14 * w, 14 * w + 14)))
+                if w == B - 1:
+                    send("s%d" % k, b * B * K, "u%d" % k, base[b] + R * B, H * B, "au%d" % k)
+
+        if k < 4:
+            rk = A("rt%d" % k, 0, R)
+            G(0); G(1)
+            if k == 1:
+                sc(rk, A("vb", 3 * R, 4 * R), -1.0, 2.0)
+            rship(k)
+            G(2); G(3); G(4); G(5)
+            P0(0); P0(1); P12(0); P0(2); P12(1); E(0)
+            P0(3); P12(2); E(1); P0(4); P12(3); E(2)
+            ship(0, 1, 2); P0(5); P12(4); E(3); G(6); P12(5); E(4); ship(3, 4); P0(6); E(5); ship(5); G(7)
+            arrive([A("u%d" % k, base[b] + R * B, base[b] + PL * B) for b in range(NB)], "au%d" % k, INC * NB)
+            G(8)
+            if k > 1:
+                sc(A("rr", R, 3 * R), IND(A("rt%d" % (k - 1), 0, PL), A("spu", 24, 72)))
+            else:
+                sc(A("d4", 0, R), A("asr", 0, R))
+            P12(6); P0(8); P0(7); P12(8); P12(7)
+            E(6)
+            if k > 1:
+                tt(A("x0", 0, R), IND(A("rt%d" % (k - 1), 0, PL), A("spu", 0, 24)), A("asr", 0, R), OP.mult)
+            tt(acc(6), acc(6), rk, OP.mult)
+            if not allv and k > 1:
+                sc(X0P, A("x0", 0, R))
+            sc(acc(6), acc(6), -1.0, 2.0)
+            if k > 1:
+                tt(A("ps", xn, xn + 2 * R), A("ps", xn, xn + 2 * R), A("rr", R, 3 * R), OP.mult)
+            tt(A("rt%d" % (k + 1), 0, R), acc(6), rk, OP.mult)
+            if k == 3:
+                nst[0] += 16
+                dma("y", (T.inv[:], []), A("rt4", 0, R), ("st", 1 << 20))
+                sc(A("rr", 0, 3 * R), IND(A("rt3", 0, PL), A("spo", 0, 72)))
+        else:
+            for s in (8, 7, 6, 0, 1, 2, 3, 4, 5):
+                G(s)
+            P0(8); P0(7); P12(8); P12(7); P0(6); E(8); P0(0); P12(6); E(7); P0(1); P12(0); E(6)
+            tt(A("yb", 0, 3 * R), IND(A("d4", 0, 3 * R), A("ivu", 0, 72)), A("rr", 0, 3 * R), OP.mult)
+            store(0, 3 * R)
+            for s in range(0, 5):
+                if s < 4:
+                    P0(s + 2)
+                P12(s + 1)
+                E(s)
+            E(5)
+
+    for k in range(1, 5):
+        sweep(k)
+    _emit(g, T, ops, [("g", "sent", nsent[0]), ("y", "st", nst[0])])

@@ -5,34 +5,40 @@ NR, R, H, PL = 8, 384, 32, 608
 K = (NR - 1) * H
 B = 3
 NB = 6 // B
-PAD, BIG = 16, 4096
+PAD = 16
+BIG = PAD + B * PL
 TL = PAD + 6 * PL
 HD, COFF = "float16", 1536
-VG = (0, 1, 2, 3, 4, 5, 6, 7, 8)
-NPE = (2, 2, 2, 2, 2, 2, 2)
-NT = (3, 3, 3, 3, 3, 3, 3, 2, 1)
+KEY = 2048
+MIDDLE = ("o3 z5 G1 z4 G7 o1 z0 o0 <r0 M1 z2 g0 a5 <r1 G5 <r2 m0 a4 G3 a0 z3 o2 b0 e0 z1 a1 M5 M3 G11 s0 M7 a2 a3 G9 "
+          "c0 e1 c1 b8 s1 e2 M11 b7 s2 b11 c2 M9 e4 e3 o6 e5 z8 s3 s4 s5 g14 o7 g13 q z7 m14 a8 m13 c3 z6 c5 a7 c4 "
+          "x w a6 b12 l")
+ORDER = {
+    1: "z1 o0 z0 o1 o3 o2 g0 M1 G3 z2 G5 z4 m0 M3 z5 G7 G11 a1 a0 b0 e0 z3 M5 M7 G9 s0 a4 a5 a2 e1 c0 c1 e2 a3 M11 "
+       "s1 s2 M9 b7 b8 e3 e4 s3 b11 e5 c2 o6 s4 z8 s5 z7 z6 c3 c4 a8 g14 a7 g13 m14 m13 b14 a6 c5 w b12",
+    2: MIDDLE,
+    3: MIDDLE,
+    4: "g14 g0 o7 <r0 z8 a8 z0 o0 m14 <r1 G1 o1 q z7 <r2 o3 m0 a7 M1 G5 z2 o2 z3 G3 x z1 a0 G7 M5 l M3 b0 e0 a1 z4 a3 "
+       "z5 a2 y M7 b4 G11 e2 a5 z6 a4 g13 o6 b8 e1 M11 b11 e3 m13 G9 M9 a6 e4 e5 b12 e6",
+}
 
 SCRATCH = {
     "shipi": ("sbuf", [128, 16], "int32"), "spoti": ("sbuf", [128, 72], "int32"),
     "colw": ("sbuf", [128, PL], "int32"), "csend": ("sbuf", [128, K], "int32"),
-    "shipu": ("sbuf", [128, 16], "uint16"), "shipo": ("sbuf", [128, 14 * 6 + 12], "uint16"),
-    "spo": ("sbuf", [128, 72], "uint16"), "spu": ("sbuf", [128, 72], "uint16"),
-    "pru": ("sbuf", [128, 72], "uint16"), "ivu": ("sbuf", [128, 72], "uint16"),
+    "shipu": ("sbuf", [128, 16], "uint16"),
+    "spu": ("sbuf", [128, 96], "uint16"), "pru": ("sbuf", [128, 72], "uint16"), "ivu": ("sbuf", [128, 72], "uint16"),
     "off": ("sbuf", [128, 648], "uint16"),
     "vb": ("sbuf", [128, 10 * R], "bfloat16"), "asr": ("sbuf", [128, 3 * R], "bfloat16"),
     "colh": ("sbuf", [128, R], HD), "ot": ("sbuf", [128, 3 * R], HD),
-    "cg": ("sbuf", [128, 3 * R], HD), "ct": ("sbuf", [128, 3 * R], HD),
+    "cg": ("sbuf", [128, 3 * R], HD), "ct": ("sbuf", [128, 3 * R], HD), "nsp": ("sbuf", [128, 216], HD),
     "ones": ("sbuf", [128, 128], "bfloat16"), "sel": ("sbuf", [128, 512], "bfloat16"),
-    "idn": ("sbuf", [128, 128], "bfloat16"), "negi": ("sbuf", [128, 128], "float32"),
-    "wm": ("sbuf", [128, 128 * 6], "bfloat16"),
+    "idn": ("sbuf", [128, 128], "bfloat16"), "cb": ("sbuf", [128, 128 * 3], "bfloat16"),
+    "cf": ("sbuf", [128, 128 * 2], "float32"), "wm": ("sbuf", [128, 128 * 6], HD),
     "o3": ("sbuf", [128, 648], "float32"), "kk": ("sbuf", [128, 144], "float32"),
     "net": ("sbuf", [128, 144], "float32"), "srt": ("sbuf", [128, 144], "float32"),
-    "pay": ("sbuf", [128, 72], "float32"), "tmp": ("sbuf", [128, 72], "float32"),
-    "ki": ("sbuf", [128, 72], "int32"), "kj": ("sbuf", [128, 72], "int32"), "kt": ("sbuf", [128, 72], "int32"),
-    "nsp": ("sbuf", [128, 216], "float32"), "n3": ("sbuf", [128, 72], "float32"), "n3i": ("sbuf", [128, 72], "int32"),
-    "pi": ("sbuf", [128, 4], "int32"), "pj": ("sbuf", [128, 4], "int32"), "pf": ("sbuf", [128, 4], "float32"),
-    "ta": ("sbuf", [128, 72], "float32"), "tb": ("sbuf", [128, 72], "float32"),
-    "ext": ("sbuf", [128, 120], "float32"), "ga": ("sbuf", [128, 72], "float32"), "gb": ("sbuf", [128, 72], "float32"),
+    "tmp": ("sbuf", [128, 72], "float32"), "tn": ("sbuf", [128, 72], "float32"),
+    "ki": ("sbuf", [128, 144], "int32"), "kp": ("sbuf", [128, 144], "int32"), "kc": ("sbuf", [128, 72], "int32"),
+    "ext": ("sbuf", [128, 120], "float32"), "ga": ("sbuf", [128, 144], "bfloat16"),
     "eq": ("sbuf", [128, 54 * 72], "bfloat16"),
     "u0": ("sbuf", [128, TL], "bfloat16"), "u1": ("sbuf", [128, TL], "float32"),
     "u2": ("sbuf", [128, TL], "float32"), "u3": ("sbuf", [128, TL], "float32"),
@@ -41,12 +47,13 @@ SCRATCH = {
     "rt1": ("sbuf", [128, PL], "float32"), "rt2": ("sbuf", [128, PL], "float32"),
     "rt3": ("sbuf", [128, PL], "float32"), "rt4": ("sbuf", [128, R], "float32"),
     "rs": ("sbuf", [128, 3 * K], "float32"),
-    "gg": ("sbuf", [128, 8 * 3 * R + R], "float32"), "pp": ("sbuf", [128, 8 * 3 * R + R], "float32"),
-    "x0": ("sbuf", [128, R], "float32"), "rr": ("sbuf", [128, 3 * R], "float32"),
+    "gg": ("sbuf", [128, 15 * R], "float32"), "pp": ("sbuf", [128, 15 * R], "float32"),
+    "pz": ("sbuf", [128, 9 * R], "float32"),
+    "x0": ("sbuf", [128, R], "float32"), "rr": ("sbuf", [128, 2 * R], "float32"),
     "d4": ("sbuf", [128, 3 * R], "float32"), "yb": ("sbuf", [128, 10 * R], "float32"),
     "ps": ("psum", [128, 4096], "float32"),
 }
-SEMAPHORES = ["ev", "es", "ep", "eg", "lship", "lspot", "lcol", "lu0", "lu1", "llow", "st", "sent", "csent",
+SEMAPHORES = ["ev", "es", "ep", "eg", "lship", "lspot", "lcol", "lu0", "lu1", "llow", "st", "sent",
               "acol", "au0", "au1", "au2", "au3", "ar1", "ar2", "ar3"]
 
 
@@ -128,6 +135,9 @@ def rank_program(g, core, T, topo):
             lo, hi, st = lo // 512 * 512, (hi + 511) // 512 * 512, 1
         return (ap, [(n, lo, hi, st)])
 
+    def PS(bank, lo, hi, st=1):
+        return A("ps", bank * 512 + lo, bank * 512 + hi, st)
+
     def IND(win, off):
         return (win[0].indirect(off[0]), win[1] + off[1])
 
@@ -140,12 +150,10 @@ def rank_program(g, core, T, topo):
         op("v", lambda: g.vector.tensor_tensor(o[0], a[0], b[0], alu), [a, b], [o])
 
     def ts(o, a, s1, o0, s2=None, o1=None):
-        col = isinstance(s1, tuple)
-        x1 = s1[0] if col else s1
         if o1 is None:
-            op("v", lambda: g.vector.tensor_scalar(o[0], a[0], x1, None, o0), [a] + ([s1] if col else []), [o])
+            op("v", lambda: g.vector.tensor_scalar(o[0], a[0], s1, None, o0), [a], [o])
         else:
-            op("v", lambda: g.vector.tensor_scalar(o[0], a[0], x1, s2, o0, o1), [a] + ([s1] if col else []), [o])
+            op("v", lambda: g.vector.tensor_scalar(o[0], a[0], s1, s2, o0, o1), [a], [o])
 
     def cp(o, a):
         op("v", lambda: g.vector.tensor_copy(o[0], a[0]), [a], [o])
@@ -156,11 +164,14 @@ def rank_program(g, core, T, topo):
     def tr(o, a):
         op("v", lambda: g.vector.transpose(o[0], a[0]), [a], [o])
 
-    def sc(o, a, scale=None, bias=None):
+    def sc(o, a, scale=None, bias=0.0):
         if scale is None:
             op("s", lambda: g.scalar.activation(o[0], a[0], AF.Copy), [a], [o])
         else:
             op("s", lambda: g.scalar.activation(o[0], a[0], AF.Identity, bias=float(bias), scale=float(scale)), [a], [o])
+
+    def gsel(o, a, pattern, base, mult):
+        op("g", lambda: g.affine_select(o[0], a[0], pattern, OP.is_equal, 0.0, base, mult), [a], [o])
 
     def mm(o, l, r, start, stop):
         op("p", lambda: g.tensor.matmul(o[0], l[0], r[0], start, stop), [l, r], [o])
@@ -179,7 +190,7 @@ def rank_program(g, core, T, topo):
     INC = 2 * len(peers)
     nsent = [0]
 
-    def send(src, s0, dst, d0, width, sem, local="sent"):
+    def send(src, s0, dst, d0, width, sem):
         trs = []
         for b, c in enumerate(peers):
             qr = T.rank_of(c)
@@ -188,22 +199,23 @@ def rank_program(g, core, T, topo):
             trs.append(RemoteDMATransfer(dst_ids=[DstId(rid=rid, pnc=pid)], dma_engine_mask=masks[c],
                                          remote_sem=T.sem[sem], src=T[src][:, s0 + b * width:s0 + (b + 1) * width],
                                          dst=T[dst][:, d0 + bb * width:d0 + (bb + 1) * width]))
-        if local == "sent":
-            nsent[0] += INC
-        tok = (local, INC) if local != "sent" else ("sent", 1 << 20)
-        return op("g", lambda: g.remote_dma_fused(trs, local_sem=T.sem[local]), [A(src, s0, s0 + 7 * width)], [], tok=tok)
+        nsent[0] += INC
+        op("g", lambda: g.remote_dma_fused(trs, local_sem=T.sem["sent"]), [A(src, s0, s0 + 7 * width)], [],
+           tok=("sent", 1 << 20))
 
     def arrive(regs, sem, val):
         op(None, None, [], regs, tok=(sem, val))
 
-    def swap(o0, src, lane, n):
+    def swap(bank, o0, src, lane, n):
         for c2 in range(2):
             for g2 in range(2):
                 k = 2 * c2 + g2
-                mm(A("ps", o0 + c2, o0 + 2 * n, 2), A("sel", 128 * k, 128 * k + 128),
+                mm(PS(bank, o0 + c2, o0 + 2 * n, 2), A("sel", 128 * k, 128 * k + 128),
                    A(src, 16 * g2 + lane, 32 * n, 32), g2 == 0, g2 == 1)
 
     base = [PAD + b * PL * B for b in range(NB)]
+    IDN, NID, WB, WR = A("idn", 0, 128), A("cb", 0, 128), A("cb", 128, 256), A("cb", 256, 384)
+    ADD, SUB = A("cf", 0, 128), A("cf", 128, 256)
 
     ms(A("colw", 0, R), 0)
     ms(A("ones", 0, 128), 1.0)
@@ -214,86 +226,82 @@ def rank_program(g, core, T, topo):
     dma("s", A("spoti", 0, 72), (T.spot[:], []), ("lspot", 16))
     dma("y", A("vb", 4 * R, 7 * R), (T.val[:, 4 * R:7 * R], []), ("lu0", 16))
     dma("s", A("vb", 7 * R, 10 * R), (T.val[:, 7 * R:10 * R], []), ("lu1", 16))
+    dma("y", A("vb", 0, 4 * R), (T.val[:, 0:4 * R], []), ("llow", 16))
+    gsel(IDN, A("ones", 0, 128), [[-1, 128]], 0, 1)
     for c2 in range(2):
         for g2 in range(2):
-            def f(c2=c2, g2=g2):
-                k = 2 * c2 + g2
-                return g.affine_select(T.sel[:, 128 * k:128 * k + 128], T.ones[:, 0:128],
-                                       [[-32, 4], [1000, 2], [-1, 16]], OP.is_equal, 0.0, -16 * c2 - 1000 * g2, 1)
-            op("g", f, [A("ones", 0, 128)], [A("sel", 128 * (2 * c2 + g2), 128 * (2 * c2 + g2) + 128)])
+            k = 2 * c2 + g2
+            gsel(A("sel", 128 * k, 128 * k + 128), A("ones", 0, 128), [[-32, 4], [1000, 2], [-1, 16]],
+                 -16 * c2 - 1000 * g2, 1)
     for n in ("u0", "u1", "u2", "u3"):
         ms(A(n, 0, PAD), 0.0)
     ms(A("o3", 504, 648), 0.0)
+    wat, parts = {1: IDN}, []
+    for w in range(6):
+        v = BIG - PAD + base[w // B] + w % B
+        parts.append([v] if v <= 2048 or v % 2 == 0 else [v - 1, 1])
+    for j, v in enumerate(sorted(set(x for p in parts for x in p) - {1})):
+        wat[v] = A("wm", 128 * j, 128 * j + 128)
+        sc(wat[v], IDN, v)
+    for o, v in ((WB, B), (NID, -1), (ADD, 1), (SUB, -1), (WR, -R)):
+        sc(o, IDN, v)
     cp(A("shipu", 0, 14), A("shipi", 0, 14))
     cp(A("csend", 0, K), IND(A("colw", 0, R), A("shipu", 0, 14)))
-    cs = send("csend", 0, "colw", R, H, "acol", local="csent")
+    send("csend", 0, "colw", R, H, "acol")
     arrive([A("colw", R, PL)], "acol", INC)
-    dma("y", A("vb", 0, 4 * R), (T.val[:, 0:4 * R], []), ("llow", 16), after=[cs])
-    op("g", lambda: g.iota(T.n3i[:, 0:72], [[0, 3], [16, 24]], 0, 1), [], [A("n3i", 0, 72)])
-    op("g", lambda: g.iota(T.pi[:, 0:1], [[0, 1]], 0, 1), [], [A("pi", 0, 1)])
-    ts(A("colh", 0, R), A("colw", 0, R), float(-COFF), OP.add)
+    sc(A("colh", 0, R), A("colw", 0, R), 1.0, -COFF)
     tr(A("ot", 0, R), A("colh", 0, R))
-    for j, lane in enumerate((0, 1, 2, 0, 1)):
-        swap(3 * 512 + 24 * j, "ot", lane, 12)
+    for t in range(3):
+        swap(3, 24 * t, "ot", t, 12)
+    swap(7, 0, "ot", 3, 12)
     tr(A("ot", R, 2 * R), A("colh", 0, R))
     tr(A("ot", 2 * R, 3 * R), A("colh", 0, R))
     for j, lane in enumerate((4, 5, 6, 7, 8, 9, 3)):
-        swap(2 * 512 + 72 * j, "ot", lane, 36)
+        swap(2, 72 * j, "ot", lane, 36)
     for t in range(3):
-        ts(A("pay", 24 * t, 24 * t + 24), A("spoti", 24 * t, 24 * t + 24), 4.0, OP.mult, float(t), OP.add)
-    tt(A("idn", 0, 128), A("sel", 0, 128), A("sel", 384, 512), OP.add)
-    ts(A("tmp", 0, 72), A("ps", 1536, 1608), float(COFF + 3), OP.add, 4096.0, OP.mult)
-    cp(A("kk", 1, 144, 2), A("ps", 1536, 1608))
-    cp(A("ext", 0, 120), A("ps", 1536, 1656))
-    tt(A("kk", 0, 144, 2), A("tmp", 0, 72), A("pay", 0, 72), OP.add)
-    for w in range(B):
-        ts(A("shipo", 14 * w, 14 * w + 14), A("shipi", 0, 14), float(B), OP.mult, float(w), OP.add)
+        sc(A("tn", 24 * t, 24 * t + 24), PS(7, 0, 24), 1.0 / NR, (COFF - rank) / NR + t * R)
+    ts(A("tmp", 0, 72), PS(3, 0, 72), float(COFF + 3), OP.add, float(KEY), OP.mult)
+    sc(A("ext", 0, 72), PS(3, 0, 72))
+    sc(A("ext", 72, 120), PS(3, 0, 48))
+    tt(A("kk", 0, 144, 2), A("tmp", 0, 72), A("spoti", 0, 72), OP.add)
+    tt(A("kk", 1, 144, 2), A("tmp", 0, 72), A("tn", 0, 72), OP.add)
     tt(A("net", 0, 48), A("kk", 0, 48), A("kk", 48, 96), OP.min)
     tt(A("net", 48, 96), A("kk", 0, 48), A("kk", 48, 96), OP.max)
-    cp(A("spo", 0, 72), A("spoti", 0, 72))
+    tt(A("ga", 0, 72), A("ext", 0, 72), A("ext", 24, 96), OP.is_gt)
     tt(A("net", 96, 144), A("net", 48, 96), A("kk", 96, 144), OP.min)
     tt(A("srt", 96, 144), A("net", 48, 96), A("kk", 96, 144), OP.max)
-    tt(A("ga", 0, 72), A("ext", 0, 72), A("ext", 24, 96), OP.is_gt)
-    tt(A("srt", 0, 48), A("net", 0, 48), A("net", 96, 144), OP.min)
-    tt(A("srt", 48, 96), A("net", 0, 48), A("net", 96, 144), OP.max)
-    tt(A("gb", 0, 72), A("ext", 0, 72), A("ext", 48, 120), OP.is_gt)
-    cp(A("ki", 0, 72), A("srt", 0, 144, 2))
-    ts(A("pj", 0, 1), A("pi", 0, 1), 112, OP.bitwise_and)
-    ts(A("kj", 0, 72), A("ki", 0, 72), 2, OP.arith_shift_right, 1023, OP.bitwise_and)
-    ts(A("kt", 0, 72), A("ki", 0, 72), 3, OP.bitwise_and)
-    cp(A("pf", 0, 1), A("pj", 0, 1))
-    cp(A("spu", 0, 72), A("kj", 0, 72))
-    tt(A("ga", 0, 72), A("ga", 0, 72), A("gb", 0, 72), OP.add)
-    ts(A("n3", 0, 72), A("n3i", 0, 72), A("pf", 0, 1), OP.subtract)
-    ts(A("ta", 0, 72), A("kt", 0, 72), float(R), OP.mult)
-    ts(A("gb", 0, 72), A("ga", 0, 72), float(R), OP.mult)
+    tt(A("ga", 72, 144), A("ext", 0, 72), A("ext", 48, 120), OP.is_gt)
+    tt(A("srt", 48, 96), A("net", 0, 48), A("net", 96, 144), OP.min)
+    tt(A("srt", 0, 48), A("net", 0, 48), A("net", 96, 144), OP.max)
+    cp(A("ki", 0, 144), A("srt", 0, 144))
+    ts(A("kp", 0, 144), A("ki", 0, 144), KEY - 1, OP.bitwise_and)
+    ts(A("kc", 0, 72), A("ki", 0, 144, 2), 11, OP.arith_shift_right)
+    cp(A("spu", 0, 72), A("kp", 0, 144, 2))
+    cp(A("pru", 0, 72), A("kp", 1, 144, 2))
     for j in range(3):
-        ts(A("nsp", 72 * j, 72 * j + 72), A("kj", 0, 72), float(-B), OP.mult, float(BIG - PAD), OP.add)
-    tt(A("tb", 0, 72), A("ta", 0, 72), A("n3", 0, 72), OP.add)
-    tt(A("ga", 0, 72), A("gb", 0, 72), A("n3", 0, 72), OP.add)
-    cp(A("o3", 504, 528), A("srt", 97, 144, 2))
-    cp(A("o3", 528, 552), A("srt", 97, 144, 2))
-    cp(A("o3", 576, 600), A("srt", 49, 96, 2))
-    cp(A("pru", 0, 72), A("tb", 0, 72))
-    cp(A("ivu", 0, 72), A("ga", 0, 72))
-    sc(A("negi", 0, 128), A("idn", 0, 128), -1.0, 0.0)
-    wts = sorted(set([BIG + b * PL * B for b in range(NB)] + list(range(2, B))))
-    wat = {1: A("idn", 0, 128)}
-    for j, v in enumerate(wts):
-        wat[v] = A("wm", 128 * j, 128 * j + 128)
-        sc(wat[v], A("idn", 0, 128), v, 0.0)
+        ts(A("nsp", 72 * j, 72 * j + 72), A("kp", 0, 144, 2), float(-PL), OP.add)
+    mm(PS(7, 72, 144), ADD, A("tn", 0, 72), True, False)
+    mm(PS(7, 72, 144), WR, A("ga", 0, 72), False, False)
+    mm(PS(7, 72, 144), WR, A("ga", 72, 144), False, True)
     for j in range(3):
-        mm(A("ps", (4 + j) * 512, (4 + j) * 512 + 216), A("negi", 0, 128), A("nsp", 0, 216), True, False)
+        mm(PS(4 + j, 0, 216), WB, A("nsp", 0, 216), True, False)
     for b in range(NB):
         for w in range(B):
             s = 4 + b * B + w
             sc(A("s0", b * B * K + w, (b + 1) * B * K, B), IND(A("vb", s * R, s * R + R), A("shipu", 0, 14)))
+    sc(A("o3", 0, 504), PS(2, 0, 504))
+    for t in range(3):
+        sc(A("ivu", 24 * t, 24 * t + 24), PS(7, 72 + 24 * t, 96 + 24 * t), 1.0, (2 - t) * R)
+
+    def own(w):
+        gsel(A("u0", base[w // B] + w % B, base[w // B] + R * B, B), A("vb", (4 + w) * R, (5 + w) * R), [[0, R]], 0, 0)
+    for w in range(3):
+        own(w)
+    for b in range(NB):
         send("s0", b * B * K, "u0", base[b] + R * B, H * B, "au0")
     arrive([A("u0", base[b] + R * B, base[b] + PL * B) for b in range(NB)], "au0", INC * NB)
-    sc(A("o3", 0, 504), A("ps", 1024, 1528))
-    for w in range(6):
-        sc(A("u0", base[w // B] + w % B, base[w // B] + R * B, B), A("vb", (4 + w) * R, (5 + w) * R))
-    sc(A("asr", 0, 3 * R), IND(A("vb", 0, 3 * R), A("pru", 0, 72)))
+    for w in range(3, 6):
+        own(w)
 
     def xb(k):
         return (k % 2) * 1024 + 128
@@ -303,37 +311,39 @@ def rank_program(g, core, T, topo):
         send("rs", (k - 1) * K, "rt%d" % k, R, H, "ar%d" % k)
         arrive([A("rt%d" % k, R, PL)], "ar%d" % k, INC)
 
-    for t in range(3):
-        ts(A("cg", t * R, t * R + R), IND(A("colw", 0, PL), A("spu", 24 * t, 24 * t + 24)), float(-COFF), OP.add)
-        if t:
-            tr(A("ct", t * R - R, t * R), A("cg", t * R - R, t * R))
+    def places(t):
+        return IND(A("colw", 0, PL), A("spu", 24 * t, 24 * t + 24))
+    ts(A("cg", 0, R), places(0), float(-COFF), OP.add)
+    for t in (1, 2):
+        sc(A("cg", t * R, t * R + R), places(t), 1.0, -COFF)
+    for o, t in ((504, 2), (528, 2), (600, 0)):
+        ts(A("o3", o, o + 24), A("kc", 24 * t, 24 * t + 24), float(-3 - COFF), OP.add)
+    tr(A("ct", 0, R), A("cg", 0, R))
+    tr(A("ct", R, 2 * R), A("cg", R, 2 * R))
+    cp(A("spu", 72, 96), A("kp", 0, 48, 2))
     tr(A("ct", 2 * R, 3 * R), A("cg", 2 * R, 3 * R))
+    sc(A("asr", 0, 3 * R), IND(A("vb", 0, 3 * R), A("pru", 0, 72)))
     for w in range(5, -1, -1):
-        swap(296 + 72 * w, "ct", 4 + w, 36)
+        swap(0, 296 + 72 * w, "ct", 4 + w, 36)
     e0 = 0
     for d in range(-5, 9):
         w0, w1 = max(0, -d), min(5, 8 - d)
         n = (w1 - w0 + 1) * 72
-        tt(A("eq", e0, e0 + n), A("o3", (d + w0) * 72, (d + w0) * 72 + n), A("ps", 296 + w0 * 72, 296 + w0 * 72 + n),
+        tt(A("eq", e0, e0 + n), A("o3", (d + w0) * 72, (d + w0) * 72 + n), PS(0, 296 + w0 * 72, 296 + w0 * 72 + n),
            OP.is_equal)
-        if d in (3, 6):
-            j = d // 3 - 1
-            cp(A("off", 216 * j, 216 * j + 216), A("ps", (4 + j) * 512, (4 + j) * 512 + 216))
         for w in range(w1, w0 - 1, -1):
             sg = d + w
-            o = A("ps", (4 + sg // 3) * 512 + (sg % 3) * 72, (4 + sg // 3) * 512 + (sg % 3) * 72 + 72)
-            rhs = A("eq", e0 + (w - w0) * 72, e0 + (w - w0) * 72 + 72)
-            if w % B:
-                mm(o, wat[w % B], rhs, False, False)
-            mm(o, wat[BIG + (w // B) * PL * B], rhs, False, w == 0 and sg % 3 == 2)
+            for v in parts[w]:
+                mm(PS(4 + sg // 3, (sg % 3) * 72, (sg % 3) * 72 + 72), wat[v],
+                   A("eq", e0 + (w - w0) * 72, e0 + (w - w0) * 72 + 72), False, w == 0 and sg % 3 == 2)
+        if d in (2, 5, 8):
+            j = d // 3
+            sc(A("off", 216 * j, 216 * j + 216), PS(4 + j, 0, 216))
+        if d == 2:
+            sc(A("gg", R, 3 * R), IND(A("u0", 0, TL), A("off", 48, 96)))
         e0 += n
-    cp(A("off", 432, 648), A("ps", 6 * 512, 6 * 512 + 216))
-    for j in range(2):
-        mm(A("ps", xb(1) + j * R, xb(1) + j * R + R), A("idn", 0, 128), A("asr", R + j * R, 2 * R + j * R), True, True)
-    allv = len(VG) == 9
-    X0P = A("ps", 7 * 512, 7 * 512 + R)
-    if not allv:
-        mm(X0P, A("idn", 0, 128), A("asr", 0, R), True, True)
+    mm(A("ps", xb(1), xb(1) + R), NID, A("asr", 2 * R, 3 * R), True, True)
+    mm(A("ps", xb(1) + R, xb(1) + 2 * R), NID, A("asr", 0, R), True, True)
     nst = [0]
 
     def store(lo, hi):
@@ -342,112 +352,116 @@ def rank_program(g, core, T, topo):
 
     def sweep(k):
         tin = A("u%d" % (k - 1), 0, TL)
-        x0 = A("asr", 0, R) if k <= 2 else A("x0", 0, R)
+        x0 = A("asr", R, 2 * R) if k <= 2 else A("x0", 0, R)
         xo, xn = xb(k), xb(k + 1)
-        nb = 4 if allv else 3
+
+        def at(s):
+            return xn + s % 3 % 2 * R if s in (4, 5) else xn + (s - 7) * R if s >= 7 else \
+                (4 + min(s // 2, 1) * 2) * 512 + 128 + s % 2 * R
 
         def acc(s):
-            c = (4 + s % nb) * 512 if s < 7 else xn + (8 - s) * R
-            return A("ps", c, c + R)
+            return A("ps", at(s), at(s) + R)
 
-        def pr(n, s, t0, t1):
-            return A(n, (3 * s + t0) * R, (3 * s + t1) * R)
+        def val(s):
+            c = (4 + s if s < 6 else 3) * R
+            return A("vb", c, c + R) if s < 7 else A("asr", (16 - 2 * s) * R, (17 - 2 * s) * R)
 
-        def G(s):
-            t0 = 1 if s in VG else 0
-            if t0 < NT[s]:
-                sc(pr("gg", s, t0, NT[s]), IND(tin, A("off", 72 * s + 24 * t0, 72 * s + 24 * NT[s])))
+        words = ORDER[k].split()
+        opened = [int(x[1:]) for x in words if x[0] == "o"]
+        added = [int(x[1:]) for x in words if x[0] == "b"]
+        direct = [j for j in range(15) if j // 2 in opened and j % 4 in (1, 2)]
+        left = {s: 1 + sum(j // 2 == s for j in added) for s in range(9)}
+        flip = k == 1
 
-        def P0(s):
-            if s in VG:
-                tt(pr("pp", s, 0, 1), IND(tin, A("off", 72 * s, 72 * s + 24)), x0, OP.mult)
-            else:
-                tt(pr("pp", s, 0, 1), pr("gg", s, 0, 1), X0P, OP.mult)
+        def pr(n, j, m=1):
+            return A(n, j * R, (j + m) * R)
 
-        def npe(s):
-            return NPE[s] if s < 7 else (NT[s] if k < 4 else NT[s] - 1)
+        def G(j, m):
+            c = 72 * (j // 2) + 48 * (j % 2)
+            sc(pr("gg", j, m), IND(tin, A("off", c, c + 24 * m)))
 
-        def PE(s):
-            a = A("vb", (4 + s) * R, (5 + s) * R) if s < 6 else (A("vb", 3 * R, 4 * R) if s == 6 else
-                                                              A("asr", (9 - s) * R, (10 - s) * R))
-            mm(acc(s), A("idn", 0, 128), a, True, npe(s) == 0)
-            for t in range(npe(s)):
-                mm(acc(s), A("negi", 0, 128), pr("pp", s, t, t + 1), False, t == npe(s) - 1)
+        def Z(s):
+            tt(pr("pz", s), IND(tin, A("off", 72 * s + 24, 72 * s + 48)), x0, OP.mult)
 
-        def P12(s):
-            if NT[s] > 1:
-                tt(pr("pp", s, 1, NT[s]), pr("gg", s, 1, NT[s]), A("ps", xo, xo + (NT[s] - 1) * R), OP.mult)
-            PE(s)
+        def M(j, m):
+            c = xo + (1 - j % 2) * R
+            o = A("ps", at(j // 2), at(j // 2) + m * R) if j in direct else pr("pp", j, m)
+            tt(o, pr("gg", j, m), A("ps", c, c + m * R), OP.mult)
+
+        def OPEN(s):
+            mm(acc(s), IDN, val(s), True, False)
+
+        def SUM(s):
+            left[s] -= 1
+            low = flip and s >= 7
+            mm(acc(s), NID if low else IDN, val(s), s not in opened, False)
+            mm(acc(s), ADD if low else SUB, pr("pz", s), False, left[s] == 0)
+
+        def MORE(j):
+            left[j // 2] -= 1
+            mm(acc(j // 2), SUB if flip and j == 14 else ADD, pr("pp", j), False, left[j // 2] == 0)
+
+        def out(s):
+            return pr("yb", 4 + s if s < 6 else 3)
 
         def E(s):
-            if s >= 7:
-                out = A("d4", (9 - s) * R, (10 - s) * R)
-            elif k == 4:
-                sl = 4 + s if s < 6 else 3
-                out = A("yb", sl * R, sl * R + R)
-            elif s < 6:
-                out = A("u%d" % k, base[s // B] + s % B, base[s // B] + R * B, B)
+            rest = [j for j in (2 * s, 2 * s + 1) if j not in direct and j not in added]
+            if rest:
+                tt(out(s), acc(s), pr("pp", rest[0]), OP.add)
             else:
-                out = acc(s)
-            for t in range(npe(s), NT[s]):
-                tt(out if t == NT[s] - 1 else acc(s), acc(s), pr("pp", s, t, t + 1), OP.subtract)
-            if npe(s) == NT[s] and (s < 6 or k == 4):
-                sc(out, acc(s))
-            if k == 4 and s < 7:
-                store(sl * R, sl * R + R)
+                sc(out(s), acc(s))
+            if k == 4:
+                store((4 + s if s < 6 else 3) * R, (5 + s if s < 6 else 4) * R)
 
-        def ship(*ss):
-            for s in ss:
-                b, w = s // B, s % B
-                sc(A("s%d" % k, b * B * K + w, (b + 1) * B * K, B),
-                   IND(A("u%d" % k, base[b], base[b] + R * B), A("shipo", 14 * w, 14 * w + 14)))
-                if w == B - 1:
-                    send("s%d" % k, b * B * K, "u%d" % k, base[b] + R * B, H * B, "au%d" % k)
+        def C(s):
+            gsel(A("u%d" % k, base[s // B] + s % B, base[s // B] + R * B, B), out(s), [[0, R]], 0, 0)
 
-        if k < 4:
-            rk = A("rt%d" % k, 0, R)
-            G(0); G(1)
-            if k == 1:
-                sc(rk, A("vb", 3 * R, 4 * R), -1.0, 2.0)
-            rship(k)
-            G(2); G(3); G(4); G(5)
-            P0(0); P0(1); P12(0); P0(2); P12(1); E(0)
-            P0(3); P12(2); E(1); P0(4); P12(3); E(2)
-            ship(0, 1, 2); P0(5); P12(4); E(3); G(6); P12(5); E(4); ship(3, 4); P0(6); E(5); ship(5); G(7)
-            arrive([A("u%d" % k, base[b] + R * B, base[b] + PL * B) for b in range(NB)], "au%d" % k, INC * NB)
-            G(8)
-            if k > 1:
-                sc(A("rr", R, 3 * R), IND(A("rt%d" % (k - 1), 0, PL), A("spu", 24, 72)))
-            else:
-                sc(A("d4", 0, R), A("asr", 0, R))
-            P12(6); P0(8); P0(7); P12(8); P12(7)
-            E(6)
-            if k > 1:
-                tt(A("x0", 0, R), IND(A("rt%d" % (k - 1), 0, PL), A("spu", 0, 24)), A("asr", 0, R), OP.mult)
-            tt(acc(6), acc(6), rk, OP.mult)
-            if not allv and k > 1:
-                sc(X0P, A("x0", 0, R))
-            sc(acc(6), acc(6), -1.0, 2.0)
-            if k > 1:
-                tt(A("ps", xn, xn + 2 * R), A("ps", xn, xn + 2 * R), A("rr", R, 3 * R), OP.mult)
-            tt(A("rt%d" % (k + 1), 0, R), acc(6), rk, OP.mult)
-            if k == 3:
-                nst[0] += 16
-                dma("y", (T.inv[:], []), A("rt4", 0, R), ("st", 1 << 20))
-                sc(A("rr", 0, 3 * R), IND(A("rt3", 0, PL), A("spo", 0, 72)))
-        else:
-            for s in (8, 7, 6, 0, 1, 2, 3, 4, 5):
-                G(s)
-            P0(8); P0(7); P12(8); P12(7); P0(6); E(8); P0(0); P12(6); E(7); P0(1); P12(0); E(6)
-            tt(A("yb", 0, 3 * R), IND(A("d4", 0, 3 * R), A("ivu", 0, 72)), A("rr", 0, 3 * R), OP.mult)
+        def S(s):
+            b, w = s // B, s % B
+            sc(A("s%d" % k, b * B * K + w, (b + 1) * B * K, B), IND(out(s), A("shipu", 0, 14)))
+            if w == B - 1:
+                send("s%d" % k, b * B * K, "u%d" % k, base[b] + R * B, H * B, "au%d" % k)
+            if s == 5:
+                arrive([A("u%d" % k, c + R * B, c + PL * B) for c in base], "au%d" % k, INC * NB)
+
+        def X(_):
+            tt(A("x0", 0, R) if k < 4 else A("d4", 2 * R, 3 * R),
+               IND(A("rt%d" % (k - 1), 0, PL), A("spu", 24, 48)), A("asr", R, 2 * R), OP.mult)
+
+        def Q(_):
+            sc(A("rr", 0, 2 * R), IND(A("rt%d" % (k - 1), 0, PL), A("spu", 48, 96)), -1.0 if k < 4 else 1.0)
+
+        def L(_):
+            tt(A("ps", xn, xn + 2 * R) if k < 4 else A("d4", 0, 2 * R), A("ps", xn, xn + 2 * R), A("rr", 0, 2 * R), OP.mult)
+
+        def Y(_):
+            sc(A("yb", 0, 3 * R), IND(A("d4", 0, 3 * R), A("ivu", 0, 72)))
             store(0, 3 * R)
-            for s in range(0, 5):
-                if s < 4:
-                    P0(s + 2)
-                P12(s + 1)
-                E(s)
-            E(5)
 
+        def RN(j):
+            rk = A("rt%d" % k, 0, R)
+            if j == 0:
+                tt(acc(6), acc(6), rk, OP.mult)
+            elif j == 1:
+                sc(acc(6), acc(6), -1.0, 2.0)
+            else:
+                tt(A("rt%d" % (k + 1), 0, R), acc(6), rk, OP.mult)
+                if k == 3:
+                    nst[0] += 16
+                    dma("y", (T.inv[:], []), A("rt4", 0, R), ("st", 1 << 20))
+
+        def W(_):
+            if k == 1:
+                sc(A("rt1", 0, R), A("vb", 3 * R, 4 * R), -1.0, 2.0)
+            rship(k)
+
+        return {"g": lambda j: G(j, 1), "G": lambda j: G(j, 2), "m": lambda j: M(j, 1), "M": lambda j: M(j, 2),
+                "z": Z, "o": OPEN, "a": SUM, "b": MORE, "e": E, "c": C, "s": S, "x": X, "q": Q, "l": L, "y": Y,
+                "r": RN, "w": W}
+
+    steps = {k: sweep(k) for k in range(1, 5)}
     for k in range(1, 5):
-        sweep(k)
+        for word in ORDER[k].split():
+            back = word[0] == "<"
+            steps[k - back][word[back]](int(word[back + 1:] or 0))
     _emit(g, T, ops, [("g", "sent", nsent[0]), ("y", "st", nst[0])])

@@ -10,16 +10,16 @@ BIG = PAD + B * PL
 TL = PAD + 6 * PL
 HD, COFF = "float16", 1536
 KEY = 2048
-MIDDLE = ("o3 z5 G1 z4 G7 o1 z0 o0 <r0 M1 z2 g0 a5 <r1 G5 <r2 m0 a4 G3 a0 z3 o2 b0 e0 z1 a1 M5 M3 G11 s0 M7 a2 a3 G9 "
-          "c0 e1 c1 b8 s1 e2 M11 b7 s2 b11 c2 M9 e4 e3 o6 e5 z8 s3 s4 s5 g14 o7 g13 q z7 m14 a8 m13 c3 z6 c5 a7 c4 "
-          "x w a6 b12 l")
 ORDER = {
-    1: "z1 o0 z0 o1 o3 o2 g0 M1 G3 z2 G5 z4 m0 M3 z5 G7 G11 a1 a0 b0 e0 z3 M5 M7 G9 s0 a4 a5 a2 e1 c0 c1 e2 a3 M11 "
-       "s1 s2 M9 b7 b8 e3 e4 s3 b11 e5 c2 o6 s4 z8 s5 z7 z6 c3 c4 a8 g14 a7 g13 m14 m13 b14 a6 c5 w b12",
-    2: MIDDLE,
-    3: MIDDLE,
-    4: "g14 g0 o7 <r0 z8 a8 z0 o0 m14 <r1 G1 o1 q z7 <r2 o3 m0 a7 M1 G5 z2 o2 z3 G3 x z1 a0 G7 M5 l M3 b0 e0 a1 z4 a3 "
-       "z5 a2 y M7 b4 G11 e2 a5 z6 a4 g13 o6 b8 e1 M11 b11 e3 m13 G9 M9 a6 e4 e5 b12 e6",
+    1: "d1 o1 d2 G5 z1 G3 G9 o0 z0 M1 o5 o4 f0 o2 o3 z2 M5 z6 G11 a0 a1 M3 z5 a2 G7 b3 e1 M9 b0 a5 e0 z4 e2 z3 M7 o6 "
+       "s1 s0 c1 M11 a4 a3 e4 o7 s2 g13 m13 c2 g14 s4 e3 a6 b12 c0 s3 e5 z7 c4 m14 s5 c5 c3 a7 w r0 r1 z8 l r2 a8 i",
+    2: "o0 o2 z0 o1 o3 z1 <k o5 G1 G3 G5 z4 G7 f0 o4 G9 M1 z2 z3 M3 a0 b0 z8 a1 M5 z5 b3 a2 M9 e0 e2 M7 G11 e1 M11 s0 "
+       "a3 s1 e3 c0 a4 a5 e4 c1 s2 z6 o7 c3 g14 o6 s3 e5 a8 m14 z7 x c2 s4 a7 s5 g13 c5 m13 a6 q c4 l b12 w",
+    3: "z1 o0 o1 G1 <k z0 <r0 o5 <r1 M1 <r2 f0 o3 G5 G3 o4 z3 z2 a0 G9 o2 M5 b0 M3 a1 M9 z4 G7 e0 a3 M7 b3 G11 c0 e1 "
+       "z5 a2 a4 e3 e2 a5 z8 o7 a8 s0 c1 M11 e4 s1 s2 c2 g14 s3 e5 c3 s4 s5 c4 o6 m14 g13 z7 c5 a7 z6 q m13 w a6 x l "
+       "b12",
+    4: "z8 g14 <k z1 <r0 G1 f0 o0 o1 <r1 o7 m14 <r2 G3 G5 z7 M1 a8 o3 q o2 z0 G9 a7 G7 z2 z6 a1 a0 M5 b0 M3 x l e0 a2 "
+       "b4 z3 o5 g13 z4 e2 M7 o4 a3 M9 y b3 G11 o6 m13 z5 a4 e3 M11 e1 a6 e4 e6 a5 h5",
 }
 
 SCRATCH = {
@@ -27,19 +27,19 @@ SCRATCH = {
     "colw": ("sbuf", [128, PL], "int32"), "csend": ("sbuf", [128, K], "int32"),
     "shipu": ("sbuf", [128, 16], "uint16"),
     "spu": ("sbuf", [128, 96], "uint16"), "pru": ("sbuf", [128, 72], "uint16"), "ivu": ("sbuf", [128, 72], "uint16"),
-    "off": ("sbuf", [128, 648], "uint16"),
+    "off": ("sbuf", [128, 576], "uint16"),
     "vb": ("sbuf", [128, 10 * R], "bfloat16"), "asr": ("sbuf", [128, 3 * R], "bfloat16"),
     "colh": ("sbuf", [128, R], HD), "ot": ("sbuf", [128, 3 * R], HD),
-    "cg": ("sbuf", [128, 3 * R], HD), "ct": ("sbuf", [128, 3 * R], HD), "nsp": ("sbuf", [128, 216], HD),
-    "ones": ("sbuf", [128, 128], "bfloat16"), "sel": ("sbuf", [128, 512], "bfloat16"),
-    "idn": ("sbuf", [128, 128], "bfloat16"), "cb": ("sbuf", [128, 128 * 3], "bfloat16"),
+    "cg": ("sbuf", [128, 3 * R], HD), "ct": ("sbuf", [128, 4 * R], HD),
+    "nsp": ("sbuf", [128, 288], HD), "low": ("sbuf", [128, 72], HD),
+    "ones": ("sbuf", [128, 256], "bfloat16"), "sel": ("sbuf", [128, 512], "bfloat16"),
+    "idn": ("sbuf", [128, 128], "bfloat16"), "cb": ("sbuf", [128, 128 * 4], "bfloat16"),
     "cf": ("sbuf", [128, 128 * 2], "float32"), "wm": ("sbuf", [128, 128 * 6], HD),
-    "o3": ("sbuf", [128, 648], "float32"), "kk": ("sbuf", [128, 144], "float32"),
-    "net": ("sbuf", [128, 144], "float32"), "srt": ("sbuf", [128, 144], "float32"),
-    "tmp": ("sbuf", [128, 72], "float32"), "tn": ("sbuf", [128, 72], "float32"),
+    "o3": ("sbuf", [128, 504], "float32"), "kk": ("sbuf", [128, 144], "float32"),
+    "net": ("sbuf", [128, 144], "float32"), "tn": ("sbuf", [128, 72], "float32"),
     "ki": ("sbuf", [128, 144], "int32"), "kp": ("sbuf", [128, 144], "int32"), "kc": ("sbuf", [128, 72], "int32"),
     "ext": ("sbuf", [128, 120], "float32"), "ga": ("sbuf", [128, 144], "bfloat16"),
-    "eq": ("sbuf", [128, 54 * 72], "bfloat16"),
+    "eq": ("sbuf", [128, 48 * 72], "bfloat16"),
     "u0": ("sbuf", [128, TL], "bfloat16"), "u1": ("sbuf", [128, TL], "float32"),
     "u2": ("sbuf", [128, TL], "float32"), "u3": ("sbuf", [128, TL], "float32"),
     "s0": ("sbuf", [128, 6 * K], "bfloat16"), "s1": ("sbuf", [128, 6 * K], "float32"),
@@ -49,7 +49,7 @@ SCRATCH = {
     "rs": ("sbuf", [128, 3 * K], "float32"),
     "gg": ("sbuf", [128, 15 * R], "float32"), "pp": ("sbuf", [128, 15 * R], "float32"),
     "pz": ("sbuf", [128, 9 * R], "float32"),
-    "x0": ("sbuf", [128, R], "float32"), "rr": ("sbuf", [128, 2 * R], "float32"),
+    "x0": ("sbuf", [128, R], "float32"), "x1": ("sbuf", [128, R], "float32"), "rr": ("sbuf", [128, 2 * R], "float32"),
     "d4": ("sbuf", [128, 3 * R], "float32"), "yb": ("sbuf", [128, 10 * R], "float32"),
     "ps": ("psum", [128, 4096], "float32"),
 }
@@ -170,6 +170,9 @@ def rank_program(g, core, T, topo):
         else:
             op("s", lambda: g.scalar.activation(o[0], a[0], AF.Identity, bias=float(bias), scale=float(scale)), [a], [o])
 
+    def fn(o, a, f, scale, bias):
+        op("s", lambda: g.scalar.activation(o[0], a[0], f, bias=bias, scale=scale), [a], [o])
+
     def gsel(o, a, pattern, base, mult):
         op("g", lambda: g.affine_select(o[0], a[0], pattern, OP.is_equal, 0.0, base, mult), [a], [o])
 
@@ -206,36 +209,38 @@ def rank_program(g, core, T, topo):
     def arrive(regs, sem, val):
         op(None, None, [], regs, tok=(sem, val))
 
-    def swap(bank, o0, src, lane, n):
+    def swap(bank, o0, src, lane, n, s0=0, onto=False):
         for c2 in range(2):
             for g2 in range(2):
                 k = 2 * c2 + g2
                 mm(PS(bank, o0 + c2, o0 + 2 * n, 2), A("sel", 128 * k, 128 * k + 128),
-                   A(src, 16 * g2 + lane, 32 * n, 32), g2 == 0, g2 == 1)
+                   A(src, s0 + 16 * g2 + lane, s0 + 32 * n, 32), g2 == 0 and not onto, k == 3 if onto else g2 == 1)
 
     base = [PAD + b * PL * B for b in range(NB)]
-    IDN, NID, WB, WR = A("idn", 0, 128), A("cb", 0, 128), A("cb", 128, 256), A("cb", 256, 384)
+    IDN = A("idn", 0, 128)
+    NID, WB, WR, NKEY = (A("cb", 128 * j, 128 * j + 128) for j in range(4))
     ADD, SUB = A("cf", 0, 128), A("cf", 128, 256)
 
     ms(A("colw", 0, R), 0)
     ms(A("ones", 0, 128), 1.0)
+    ms(A("ones", 128, 256), float(KEY))
     dma("y", A("shipi", 0, 14), (T.ship[:], []), ("lship", 16))
+    dma("s", A("spoti", 0, 72), (T.spot[:], []), ("lspot", 16))
     for gi in range(8):
         dma("y" if gi % 2 == 0 else "s", (T.colw[16 * gi:16 * gi + 10, 0:R], [("colw", 0, R, 1)]),
             (T.col[gi:gi + 1, :], []), ("lcol", 128))
-    dma("s", A("spoti", 0, 72), (T.spot[:], []), ("lspot", 16))
     dma("y", A("vb", 4 * R, 7 * R), (T.val[:, 4 * R:7 * R], []), ("lu0", 16))
     dma("s", A("vb", 7 * R, 10 * R), (T.val[:, 7 * R:10 * R], []), ("lu1", 16))
-    dma("y", A("vb", 0, 4 * R), (T.val[:, 0:4 * R], []), ("llow", 16))
     gsel(IDN, A("ones", 0, 128), [[-1, 128]], 0, 1)
     for c2 in range(2):
         for g2 in range(2):
             k = 2 * c2 + g2
-            gsel(A("sel", 128 * k, 128 * k + 128), A("ones", 0, 128), [[-32, 4], [1000, 2], [-1, 16]],
+            gsel(A("sel", 128 * k, 128 * k + 128), A("ones", 128, 256), [[-32, 4], [1000, 2], [-1, 16]],
                  -16 * c2 - 1000 * g2, 1)
     for n in ("u0", "u1", "u2", "u3"):
         ms(A(n, 0, PAD), 0.0)
-    ms(A("o3", 504, 648), 0.0)
+    for o, v in ((NID, -1), (ADD, 1), (SUB, -1), (WR, -R), (NKEY, -KEY)):
+        ts(o, IDN, float(v), OP.mult)
     wat, parts = {1: IDN}, []
     for w in range(6):
         v = BIG - PAD + base[w // B] + w % B
@@ -243,55 +248,39 @@ def rank_program(g, core, T, topo):
     for j, v in enumerate(sorted(set(x for p in parts for x in p) - {1})):
         wat[v] = A("wm", 128 * j, 128 * j + 128)
         sc(wat[v], IDN, v)
-    for o, v in ((WB, B), (NID, -1), (ADD, 1), (SUB, -1), (WR, -R)):
-        sc(o, IDN, v)
+    sc(WB, IDN, B)
     cp(A("shipu", 0, 14), A("shipi", 0, 14))
     cp(A("csend", 0, K), IND(A("colw", 0, R), A("shipu", 0, 14)))
     send("csend", 0, "colw", R, H, "acol")
     arrive([A("colw", R, PL)], "acol", INC)
     sc(A("colh", 0, R), A("colw", 0, R), 1.0, -COFF)
     tr(A("ot", 0, R), A("colh", 0, R))
+    swap(7, 0, "ot", 3, 12)
     for t in range(3):
         swap(3, 24 * t, "ot", t, 12)
-    swap(7, 0, "ot", 3, 12)
     tr(A("ot", R, 2 * R), A("colh", 0, R))
     tr(A("ot", 2 * R, 3 * R), A("colh", 0, R))
     for j, lane in enumerate((4, 5, 6, 7, 8, 9, 3)):
         swap(2, 72 * j, "ot", lane, 36)
     for t in range(3):
-        sc(A("tn", 24 * t, 24 * t + 24), PS(7, 0, 24), 1.0 / NR, (COFF - rank) / NR + t * R)
-    ts(A("tmp", 0, 72), PS(3, 0, 72), float(COFF + 3), OP.add, float(KEY), OP.mult)
-    sc(A("ext", 0, 72), PS(3, 0, 72))
-    sc(A("ext", 72, 120), PS(3, 0, 48))
-    tt(A("kk", 0, 144, 2), A("tmp", 0, 72), A("spoti", 0, 72), OP.add)
-    tt(A("kk", 1, 144, 2), A("tmp", 0, 72), A("tn", 0, 72), OP.add)
+        sc(A("tn", 24 * t, 24 * t + 24), PS(7, 0, 24), 1.0 / (NR * KEY), (COFF - rank) / NR + t * R)
+    tt(A("kk", 0, 144, 2), PS(3, 0, 72), A("spoti", 0, 72), OP.add)
+    tt(A("kk", 1, 144, 2), PS(3, 0, 72), A("tn", 0, 72), OP.add)
     tt(A("net", 0, 48), A("kk", 0, 48), A("kk", 48, 96), OP.min)
     tt(A("net", 48, 96), A("kk", 0, 48), A("kk", 48, 96), OP.max)
-    tt(A("ga", 0, 72), A("ext", 0, 72), A("ext", 24, 96), OP.is_gt)
+    tt(A("ki", 96, 144), A("net", 48, 96), A("kk", 96, 144), OP.max)
     tt(A("net", 96, 144), A("net", 48, 96), A("kk", 96, 144), OP.min)
-    tt(A("srt", 96, 144), A("net", 48, 96), A("kk", 96, 144), OP.max)
-    tt(A("ga", 72, 144), A("ext", 0, 72), A("ext", 48, 120), OP.is_gt)
-    tt(A("srt", 48, 96), A("net", 0, 48), A("net", 96, 144), OP.min)
-    tt(A("srt", 0, 48), A("net", 0, 48), A("net", 96, 144), OP.max)
-    cp(A("ki", 0, 144), A("srt", 0, 144))
+    dma("y", A("vb", 0, 4 * R), (T.val[:, 0:4 * R], []), ("llow", 16), after=[len(ops) - 1])
+    tt(A("ki", 48, 96), A("net", 0, 48), A("net", 96, 144), OP.min)
+    tt(A("ki", 0, 48), A("net", 0, 48), A("net", 96, 144), OP.max)
     ts(A("kp", 0, 144), A("ki", 0, 144), KEY - 1, OP.bitwise_and)
     ts(A("kc", 0, 72), A("ki", 0, 144, 2), 11, OP.arith_shift_right)
     cp(A("spu", 0, 72), A("kp", 0, 144, 2))
-    cp(A("pru", 0, 72), A("kp", 1, 144, 2))
-    for j in range(3):
-        ts(A("nsp", 72 * j, 72 * j + 72), A("kp", 0, 144, 2), float(-PL), OP.add)
-    mm(PS(7, 72, 144), ADD, A("tn", 0, 72), True, False)
-    mm(PS(7, 72, 144), WR, A("ga", 0, 72), False, False)
-    mm(PS(7, 72, 144), WR, A("ga", 72, 144), False, True)
-    for j in range(3):
-        mm(PS(4 + j, 0, 216), WB, A("nsp", 0, 216), True, False)
+    cp(A("o3", 0, 504), PS(2, 0, 504))
     for b in range(NB):
         for w in range(B):
             s = 4 + b * B + w
             sc(A("s0", b * B * K + w, (b + 1) * B * K, B), IND(A("vb", s * R, s * R + R), A("shipu", 0, 14)))
-    sc(A("o3", 0, 504), PS(2, 0, 504))
-    for t in range(3):
-        sc(A("ivu", 24 * t, 24 * t + 24), PS(7, 72 + 24 * t, 96 + 24 * t), 1.0, (2 - t) * R)
 
     def own(w):
         gsel(A("u0", base[w // B] + w % B, base[w // B] + R * B, B), A("vb", (4 + w) * R, (5 + w) * R), [[0, R]], 0, 0)
@@ -316,31 +305,60 @@ def rank_program(g, core, T, topo):
     ts(A("cg", 0, R), places(0), float(-COFF), OP.add)
     for t in (1, 2):
         sc(A("cg", t * R, t * R + R), places(t), 1.0, -COFF)
-    for o, t in ((504, 2), (528, 2), (600, 0)):
-        ts(A("o3", o, o + 24), A("kc", 24 * t, 24 * t + 24), float(-3 - COFF), OP.add)
-    tr(A("ct", 0, R), A("cg", 0, R))
-    tr(A("ct", R, 2 * R), A("cg", R, 2 * R))
-    cp(A("spu", 72, 96), A("kp", 0, 48, 2))
-    tr(A("ct", 2 * R, 3 * R), A("cg", 2 * R, 3 * R))
+    sc(A("ext", 0, 72), PS(3, 0, 72))
+    sc(A("ext", 72, 120), PS(3, 0, 48))
+    cp(A("pru", 0, 72), A("kp", 1, 144, 2))
+    for t in range(3):
+        ts(A("low", 24 * t, 24 * t + 24), A("kc", 48 * (t > 0), 48 * (t > 0) + 24), 1.0, OP.mult)
+        tr(A("ct", t * R + R, t * R + 2 * R), A("cg", t * R, t * R + R))
+    for j in range(3):
+        ts(A("nsp", 72 * j, 72 * j + 72), A("kp", 0, 144, 2), float(-PL), OP.add)
+    sc(A("ct", 0, R), A("ct", 2 * R, 3 * R))
+    sc(A("nsp", 216, 240), A("kp", 48, 96, 2), 1.0, -PL)
+    sc(A("nsp", 240, 288), A("kp", 0, 96, 2), 1.0, -PL)
     sc(A("asr", 0, 3 * R), IND(A("vb", 0, 3 * R), A("pru", 0, 72)))
     for w in range(5, -1, -1):
-        swap(0, 296 + 72 * w, "ct", 4 + w, 36)
+        swap(0, 296 + 72 * w, "ct", 4 + w, 36, R)
+    tt(A("ga", 0, 72), A("ext", 0, 72), A("ext", 24, 96), OP.is_gt)
+    tt(A("ga", 72, 144), A("ext", 0, 72), A("ext", 48, 120), OP.is_gt)
+    for bank, lo, hi in ((4, 0, 144), (5, 0, 216), (6, 72, 288)):
+        mm(PS(bank, 0, hi - lo), WB, A("nsp", lo, hi), True, False)
+    for w in range(6):
+        mm(PS(2, 72 * w, 72 * w + 72), NKEY, A("low", 0, 72), True, False)
+        swap(2, 72 * w, "ct", 4 + w, 36, 0, True)
+    fn(PS(2, 0, 432), PS(2, 0, 432), AF.Abs, 1.0, 0.0)
+    fn(A("eq", 42 * 72, 48 * 72), PS(2, 0, 432), AF.Relu, -1.0, 1.0)
+
+    def weigh(sg, w, e, stop):
+        c = (sg + 1) % 3 * 72 - 72 * (sg < 2)
+        for v in parts[w]:
+            mm(PS(4 + (sg + 1) // 3, c, c + 72), wat[v], A("eq", e, e + 72), False, stop)
+
+    def lists(j):
+        sc(A("off", max(216 * j - 72, 0), 216 * j + 144), PS(4 + j, 0, 216 if j else 144))
+
+    def later(_):
+        for t in range(3):
+            sc(A("ivu", 24 * t, 24 * t + 24), PS(3, 400 + 24 * t, 424 + 24 * t), 1.0, (2 - t) * R)
+        sc(A("spu", 72, 96), A("kp", 0, 48, 2))
     e0 = 0
-    for d in range(-5, 9):
-        w0, w1 = max(0, -d), min(5, 8 - d)
+    for d in range(-5, 7):
+        w0, w1 = max(0, -d), min(5, 6 - d)
         n = (w1 - w0 + 1) * 72
         tt(A("eq", e0, e0 + n), A("o3", (d + w0) * 72, (d + w0) * 72 + n), PS(0, 296 + w0 * 72, 296 + w0 * 72 + n),
            OP.is_equal)
         for w in range(w1, w0 - 1, -1):
-            sg = d + w
-            for v in parts[w]:
-                mm(PS(4 + sg // 3, (sg % 3) * 72, (sg % 3) * 72 + 72), wat[v],
-                   A("eq", e0 + (w - w0) * 72, e0 + (w - w0) * 72 + 72), False, w == 0 and sg % 3 == 2)
-        if d in (2, 5, 8):
-            j = d // 3
-            sc(A("off", 216 * j, 216 * j + 216), PS(4 + j, 0, 216))
-        if d == 2:
+            weigh(d + w, w, e0 + (w - w0) * 72, w == 0 and d in (1, 4, 6))
+        if d == -1:
+            mm(PS(3, 400, 472), ADD, A("tn", 0, 72), True, False)
+            mm(PS(3, 400, 472), WR, A("ga", 0, 72), False, False)
+            mm(PS(3, 400, 472), WR, A("ga", 72, 144), False, True)
+        if d == 1:
+            lists(0)
             sc(A("gg", R, 3 * R), IND(A("u0", 0, TL), A("off", 48, 96)))
+        if d == 4:
+            for w in range(6):
+                weigh(7, w, (42 + w) * 72, False)
         e0 += n
     mm(A("ps", xb(1), xb(1) + R), NID, A("asr", 2 * R, 3 * R), True, True)
     mm(A("ps", xb(1) + R, xb(1) + 2 * R), NID, A("asr", 0, R), True, True)
@@ -356,8 +374,10 @@ def rank_program(g, core, T, topo):
         xo, xn = xb(k), xb(k + 1)
 
         def at(s):
-            return xn + s % 3 % 2 * R if s in (4, 5) else xn + (s - 7) * R if s >= 7 else \
-                (4 + min(s // 2, 1) * 2) * 512 + 128 + s % 2 * R
+            if s >= 7:
+                return xn + (s - 7) * R
+            pair = {0: 0 if k < 4 else 4, 1: 6, 2: 4 if k < 4 else 0, 3: 6}[s // 2]
+            return (pair * 512 + 128 if pair else xn) + s % 2 * R
 
         def acc(s):
             return A("ps", at(s), at(s) + R)
@@ -369,6 +389,7 @@ def rank_program(g, core, T, topo):
         words = ORDER[k].split()
         opened = [int(x[1:]) for x in words if x[0] == "o"]
         added = [int(x[1:]) for x in words if x[0] == "b"]
+        fused = [int(x[1:]) for x in words if x[0] == "f"]
         direct = [j for j in range(15) if j // 2 in opened and j % 4 in (1, 2)]
         left = {s: 1 + sum(j // 2 == s for j in added) for s in range(9)}
         flip = k == 1
@@ -377,29 +398,37 @@ def rank_program(g, core, T, topo):
             return A(n, j * R, (j + m) * R)
 
         def G(j, m):
-            c = 72 * (j // 2) + 48 * (j % 2)
+            c = 72 * (j // 2) + 48 * (j % 2) + 24 * (j == 14)
             sc(pr("gg", j, m), IND(tin, A("off", c, c + 24 * m)))
 
         def Z(s):
-            tt(pr("pz", s), IND(tin, A("off", 72 * s + 24, 72 * s + 48)), x0, OP.mult)
+            c = 72 * s + 24 if s < 7 else 552 if s == 7 else 504
+            tt(pr("pz", s), IND(tin, A("off", c, c + 24)), x0, OP.mult)
 
         def M(j, m):
             c = xo + (1 - j % 2) * R
             o = A("ps", at(j // 2), at(j // 2) + m * R) if j in direct else pr("pp", j, m)
             tt(o, pr("gg", j, m), A("ps", c, c + m * R), OP.mult)
 
+        def F(j):
+            c = 72 * (j // 2) + 48 * (j % 2)
+            tt(pr("pp", j), IND(tin, A("off", c, c + 24)), pr("asr", 2 * (j % 2)) if flip else pr("x1", 0), OP.mult)
+
+        def KEEP(_):
+            sc(A("x1", 0, R), acc(8))
+
         def OPEN(s):
             mm(acc(s), IDN, val(s), True, False)
 
         def SUM(s):
             left[s] -= 1
-            low = flip and s >= 7
+            low = flip and s == 8
             mm(acc(s), NID if low else IDN, val(s), s not in opened, False)
             mm(acc(s), ADD if low else SUB, pr("pz", s), False, left[s] == 0)
 
         def MORE(j):
             left[j // 2] -= 1
-            mm(acc(j // 2), SUB if flip and j == 14 else ADD, pr("pp", j), False, left[j // 2] == 0)
+            mm(acc(j // 2), SUB if flip and j in fused else ADD, pr("pp", j), False, left[j // 2] == 0)
 
         def out(s):
             return pr("yb", 4 + s if s < 6 else 3)
@@ -407,11 +436,17 @@ def rank_program(g, core, T, topo):
         def E(s):
             rest = [j for j in (2 * s, 2 * s + 1) if j not in direct and j not in added]
             if rest:
-                tt(out(s), acc(s), pr("pp", rest[0]), OP.add)
+                tt(out(s), acc(s), pr("pp", rest[0]), OP.subtract if flip and rest[0] in fused else OP.add)
             else:
                 sc(out(s), acc(s))
             if k == 4:
                 store((4 + s if s < 6 else 3) * R, (5 + s if s < 6 else 4) * R)
+
+        def HALVES(s):
+            for lo in (0, R // 2):
+                c, p = (4 + s) * R + lo, (2 * s + (s in opened)) * R + lo
+                tt(A("yb", c, c + R // 2), A("ps", at(s) + lo, at(s) + lo + R // 2), A("pp", p, p + R // 2), OP.add)
+                store(c, c + R // 2)
 
         def C(s):
             gsel(A("u%d" % k, base[s // B] + s % B, base[s // B] + R * B, B), out(s), [[0, R]], 0, 0)
@@ -432,6 +467,8 @@ def rank_program(g, core, T, topo):
             sc(A("rr", 0, 2 * R), IND(A("rt%d" % (k - 1), 0, PL), A("spu", 48, 96)), -1.0 if k < 4 else 1.0)
 
         def L(_):
+            if flip:
+                return sc(acc(7), acc(7), -1.0)
             tt(A("ps", xn, xn + 2 * R) if k < 4 else A("d4", 0, 2 * R), A("ps", xn, xn + 2 * R), A("rr", 0, 2 * R), OP.mult)
 
         def Y(_):
@@ -457,7 +494,7 @@ def rank_program(g, core, T, topo):
 
         return {"g": lambda j: G(j, 1), "G": lambda j: G(j, 2), "m": lambda j: M(j, 1), "M": lambda j: M(j, 2),
                 "z": Z, "o": OPEN, "a": SUM, "b": MORE, "e": E, "c": C, "s": S, "x": X, "q": Q, "l": L, "y": Y,
-                "r": RN, "w": W}
+                "r": RN, "w": W, "f": F, "k": KEEP, "d": lists, "i": later, "h": HALVES}
 
     steps = {k: sweep(k) for k in range(1, 5)}
     for k in range(1, 5):

from concourse.bass import DstId, RemoteDMATransfer
from concourse.mybir import AluOpType as OP, ActivationFunctionType as AF

NR, R, H, PL = 8, 384, 32, 608
K = (NR - 1) * H
B = 3
NB = 6 // B
PAD = 16
BIG = PAD + B * PL
TL = PAD + 6 * PL
HD, COFF = "float16", 1536
KEY = 2048
ORDER = {
    1: "d1 o1 d2 G5 z1 G3 G9 o0 z0 M1 o5 o4 f0 o2 o3 z2 M5 z6 G11 a0 a1 M3 z5 a2 G7 b3 e1 M9 b0 a5 e0 z4 e2 z3 M7 o6 "
       "s1 s0 c1 M11 a4 a3 e4 o7 s2 g13 m13 c2 g14 s4 e3 a6 b12 c0 s3 e5 z7 c4 m14 s5 c5 c3 a7 w r0 r1 z8 l r2 a8 i",
    2: "o0 o2 z0 o1 o3 z1 <k o5 G1 G3 G5 z4 G7 f0 o4 G9 M1 z2 z3 M3 a0 b0 z8 a1 M5 z5 b3 a2 M9 e0 e2 M7 G11 e1 M11 s0 "
       "a3 s1 e3 c0 a4 a5 e4 c1 s2 z6 o7 c3 g14 o6 s3 e5 a8 m14 z7 x c2 s4 a7 s5 g13 c5 m13 a6 q c4 l b12 w",
    3: "z1 o0 o1 G1 <k z0 <r0 o5 <r1 M1 <r2 f0 o3 G5 G3 o4 z3 z2 a0 G9 o2 M5 b0 M3 a1 M9 z4 G7 e0 a3 M7 b3 G11 c0 e1 "
       "z5 a2 a4 e3 e2 a5 z8 o7 a8 s0 c1 M11 e4 s1 s2 c2 g14 s3 e5 c3 s4 s5 c4 o6 m14 g13 z7 c5 a7 z6 q m13 w a6 x l "
       "b12",
    4: "z8 g14 <k z1 <r0 G1 f0 o0 o1 <r1 o7 m14 <r2 G3 G5 z7 M1 a8 o3 q o2 z0 G9 a7 G7 z2 z6 a1 a0 M5 b0 M3 x l e0 a2 "
       "b4 z3 o5 g13 z4 e2 M7 o4 a3 M9 y b3 G11 o6 m13 z5 a4 e3 M11 e1 a6 e4 e6 a5 h5",
}

SCRATCH = {
    "shipi": ("sbuf", [128, 16], "int32"), "spoti": ("sbuf", [128, 72], "int32"),
    "colw": ("sbuf", [128, PL], "int32"), "csend": ("sbuf", [128, K], "int32"),
    "shipu": ("sbuf", [128, 16], "uint16"),
    "spu": ("sbuf", [128, 96], "uint16"), "pru": ("sbuf", [128, 72], "uint16"), "ivu": ("sbuf", [128, 72], "uint16"),
    "off": ("sbuf", [128, 576], "uint16"),
    "vb": ("sbuf", [128, 10 * R], "bfloat16"), "asr": ("sbuf", [128, 3 * R], "bfloat16"),
    "colh": ("sbuf", [128, R], HD), "ot": ("sbuf", [128, 3 * R], HD),
    "cg": ("sbuf", [128, 3 * R], HD), "ct": ("sbuf", [128, 4 * R], HD),
    "nsp": ("sbuf", [128, 288], HD), "low": ("sbuf", [128, 72], HD),
    "ones": ("sbuf", [128, 256], "bfloat16"), "sel": ("sbuf", [128, 512], "bfloat16"),
    "idn": ("sbuf", [128, 128], "bfloat16"), "cb": ("sbuf", [128, 128 * 4], "bfloat16"),
    "cf": ("sbuf", [128, 128 * 2], "float32"), "wm": ("sbuf", [128, 128 * 6], HD),
    "o3": ("sbuf", [128, 504], "float32"), "kk": ("sbuf", [128, 144], "float32"),
    "net": ("sbuf", [128, 144], "float32"), "tn": ("sbuf", [128, 72], "float32"),
    "ki": ("sbuf", [128, 144], "int32"), "kp": ("sbuf", [128, 144], "int32"), "kc": ("sbuf", [128, 72], "int32"),
    "ext": ("sbuf", [128, 120], "float32"), "ga": ("sbuf", [128, 144], "bfloat16"),
    "eq": ("sbuf", [128, 48 * 72], "bfloat16"),
    "u0": ("sbuf", [128, TL], "bfloat16"), "u1": ("sbuf", [128, TL], "float32"),
    "u2": ("sbuf", [128, TL], "float32"), "u3": ("sbuf", [128, TL], "float32"),
    "s0": ("sbuf", [128, 6 * K], "bfloat16"), "s1": ("sbuf", [128, 6 * K], "float32"),
    "s2": ("sbuf", [128, 6 * K], "float32"), "s3": ("sbuf", [128, 6 * K], "float32"),
    "rt1": ("sbuf", [128, PL], "float32"), "rt2": ("sbuf", [128, PL], "float32"),
    "rt3": ("sbuf", [128, PL], "float32"), "rt4": ("sbuf", [128, R], "float32"),
    "rs": ("sbuf", [128, 3 * K], "float32"),
    "gg": ("sbuf", [128, 15 * R], "float32"), "pp": ("sbuf", [128, 15 * R], "float32"),
    "pz": ("sbuf", [128, 9 * R], "float32"),
    "x0": ("sbuf", [128, R], "float32"), "x1": ("sbuf", [128, R], "float32"), "rr": ("sbuf", [128, 2 * R], "float32"),
    "d4": ("sbuf", [128, 3 * R], "float32"), "yb": ("sbuf", [128, 10 * R], "float32"),
    "ps": ("psum", [128, 4096], "float32"),
}
SEMAPHORES = ["ev", "es", "ep", "eg", "lship", "lspot", "lcol", "lu0", "lu1", "llow", "st", "sent",
              "acol", "au0", "au1", "au2", "au3", "ar1", "ar2", "ar3"]


def _clash(a, b, any_use):
    for n, lo, hi, st in a:
        for m, l2, h2, s2 in b:
            if n == m and lo < h2 and l2 < hi and (n == "ps" or not any_use):
                if st == 1 or st != s2 or (lo - l2) % st == 0:
                    return True
    return False


def _emit(g, T, ops, tail):
    q = {"v": g.vector, "s": g.scalar, "p": g.tensor, "g": g, "y": g.sync}
    known = {e: {} for e in q}
    seq = {e: 0 for e in q}
    need = {e: set() for e in q}
    for i, o in enumerate(ops):
        e = o["e"]
        if e is None:
            o["clock"] = {o["tok"][0]: o["tok"][1]}
            continue
        waits = []
        for d in range(i - 1, -1, -1):
            p = ops[d]
            key, val = p["tok"]
            if known[e].get(key, 0) >= val:
                continue
            if e == "p" and key == "p":
                continue
            if o["tok"] is not None and key == o["tok"][0]:
                continue
            hit = _clash(o["r"], p["w"], False) or _clash(o["w"], p["w"], False) or _clash(o["w"], p["r"], False)
            if not hit and p["e"] != e:
                hit = _clash(o["r"], p["r"], True)
            if hit or d in o["after"]:
                waits.append((key, val))
                for k2, v2 in p["clock"].items():
                    known[e][k2] = max(known[e].get(k2, 0), v2)
        o["waits"] = waits
        for key, val in waits:
            if key in need:
                need[key].add(val)
        if o["tok"] is None:
            seq[e] += 1
            o["tok"] = (e, seq[e])
        o["clock"] = dict(known[e])
        o["clock"][o["tok"][0]] = max(o["tok"][1], o["clock"].get(o["tok"][0], 0))
    count = {e: {v: j + 1 for j, v in enumerate(sorted(need[e]))} for e in need}
    for o in ops:
        e = o["e"]
        if e is None:
            continue
        for key, val in o["waits"]:
            if key in count:
                q[e].wait_ge(T.sem["e" + key], count[key][val])
            else:
                q[e].wait_ge(T.sem[key], val)
        ins = o["f"]()
        key, val = o["tok"]
        if key in count:
            if val in count[key]:
                ins.then_inc(T.sem["e" + key], 1)
        elif o["inc"]:
            ins.then_inc(T.sem[key], 16)
    for e, key, val in tail:
        q[e].wait_ge(T.sem[key], val)


def rank_program(g, core, T, topo):
    rank = T.rank_of(core)
    if rank is None:
        return
    ops = []

    def A(n, lo, hi, st=1):
        ap = T[n][:, lo:hi:st] if st > 1 else T[n][:, lo:hi]
        if n == "ps":
            lo, hi, st = lo // 512 * 512, (hi + 511) // 512 * 512, 1
        return (ap, [(n, lo, hi, st)])

    def PS(bank, lo, hi, st=1):
        return A("ps", bank * 512 + lo, bank * 512 + hi, st)

    def IND(win, off):
        return (win[0].indirect(off[0]), win[1] + off[1])

    def op(e, f, r, w, tok=None, inc=False, after=()):
        ops.append({"e": e, "f": f, "r": [x for a in r for x in a[1]], "w": [x for a in w for x in a[1]],
                    "tok": tok, "inc": inc, "after": set(after)})
        return len(ops) - 1

    def tt(o, a, b, alu):
        op("v", lambda: g.vector.tensor_tensor(o[0], a[0], b[0], alu), [a, b], [o])

    def ts(o, a, s1, o0, s2=None, o1=None):
        if o1 is None:
            op("v", lambda: g.vector.tensor_scalar(o[0], a[0], s1, None, o0), [a], [o])
        else:
            op("v", lambda: g.vector.tensor_scalar(o[0], a[0], s1, s2, o0, o1), [a], [o])

    def cp(o, a):
        op("v", lambda: g.vector.tensor_copy(o[0], a[0]), [a], [o])

    def ms(o, c):
        op("v", lambda: g.vector.memset(o[0], c), [], [o])

    def tr(o, a):
        op("v", lambda: g.vector.transpose(o[0], a[0]), [a], [o])

    def sc(o, a, scale=None, bias=0.0):
        if scale is None:
            op("s", lambda: g.scalar.activation(o[0], a[0], AF.Copy), [a], [o])
        else:
            op("s", lambda: g.scalar.activation(o[0], a[0], AF.Identity, bias=float(bias), scale=float(scale)), [a], [o])

    def fn(o, a, f, scale, bias):
        op("s", lambda: g.scalar.activation(o[0], a[0], f, bias=bias, scale=scale), [a], [o])

    def gsel(o, a, pattern, base, mult):
        op("g", lambda: g.affine_select(o[0], a[0], pattern, OP.is_equal, 0.0, base, mult), [a], [o])

    def mm(o, l, r, start, stop):
        op("p", lambda: g.tensor.matmul(o[0], l[0], r[0], start, stop), [l, r], [o])

    def dma(e, o, a, tok, after=()):
        qq = g.sync if e == "y" else g.scalar
        op(e, lambda: qq.dma_start(o[0], a[0]), [a], [o], tok=tok, inc=True, after=after)

    peers = [c for c in T.cores if c != core]
    masks, used = {}, [0, 0]
    for c in peers:
        far = 0 if topo.die(c) != topo.die(core) else 1
        eng = topo.engines(core, c)[far::2][used[far]:used[far] + 2]
        used[far] += 2
        masks[c] = (1 << eng[0]) | (1 << eng[1])
    INC = 2 * len(peers)
    nsent = [0]

    def send(src, s0, dst, d0, width, sem):
        trs = []
        for b, c in enumerate(peers):
            qr = T.rank_of(c)
            bb = rank if rank < qr else rank - 1
            rid, pid, _ = topo.addr(c)
            trs.append(RemoteDMATransfer(dst_ids=[DstId(rid=rid, pnc=pid)], dma_engine_mask=masks[c],
                                         remote_sem=T.sem[sem], src=T[src][:, s0 + b * width:s0 + (b + 1) * width],
                                         dst=T[dst][:, d0 + bb * width:d0 + (bb + 1) * width]))
        nsent[0] += INC
        op("g", lambda: g.remote_dma_fused(trs, local_sem=T.sem["sent"]), [A(src, s0, s0 + 7 * width)], [],
           tok=("sent", 1 << 20))

    def arrive(regs, sem, val):
        op(None, None, [], regs, tok=(sem, val))

    def swap(bank, o0, src, lane, n, s0=0, onto=False):
        for c2 in range(2):
            for g2 in range(2):
                k = 2 * c2 + g2
                mm(PS(bank, o0 + c2, o0 + 2 * n, 2), A("sel", 128 * k, 128 * k + 128),
                   A(src, s0 + 16 * g2 + lane, s0 + 32 * n, 32), g2 == 0 and not onto, k == 3 if onto else g2 == 1)

    base = [PAD + b * PL * B for b in range(NB)]
    IDN = A("idn", 0, 128)
    NID, WB, WR, NKEY = (A("cb", 128 * j, 128 * j + 128) for j in range(4))
    ADD, SUB = A("cf", 0, 128), A("cf", 128, 256)

    ms(A("colw", 0, R), 0)
    ms(A("ones", 0, 128), 1.0)
    ms(A("ones", 128, 256), float(KEY))
    dma("y", A("shipi", 0, 14), (T.ship[:], []), ("lship", 16))
    dma("s", A("spoti", 0, 72), (T.spot[:], []), ("lspot", 16))
    for gi in range(8):
        dma("y" if gi % 2 == 0 else "s", (T.colw[16 * gi:16 * gi + 10, 0:R], [("colw", 0, R, 1)]),
            (T.col[gi:gi + 1, :], []), ("lcol", 128))
    dma("y", A("vb", 4 * R, 7 * R), (T.val[:, 4 * R:7 * R], []), ("lu0", 16))
    dma("s", A("vb", 7 * R, 10 * R), (T.val[:, 7 * R:10 * R], []), ("lu1", 16))
    gsel(IDN, A("ones", 0, 128), [[-1, 128]], 0, 1)
    for c2 in range(2):
        for g2 in range(2):
            k = 2 * c2 + g2
            gsel(A("sel", 128 * k, 128 * k + 128), A("ones", 128, 256), [[-32, 4], [1000, 2], [-1, 16]],
                 -16 * c2 - 1000 * g2, 1)
    for n in ("u0", "u1", "u2", "u3"):
        ms(A(n, 0, PAD), 0.0)
    for o, v in ((NID, -1), (ADD, 1), (SUB, -1), (WR, -R), (NKEY, -KEY)):
        ts(o, IDN, float(v), OP.mult)
    wat, parts = {1: IDN}, []
    for w in range(6):
        v = BIG - PAD + base[w // B] + w % B
        parts.append([v] if v <= 2048 or v % 2 == 0 else [v - 1, 1])
    for j, v in enumerate(sorted(set(x for p in parts for x in p) - {1})):
        wat[v] = A("wm", 128 * j, 128 * j + 128)
        sc(wat[v], IDN, v)
    sc(WB, IDN, B)
    cp(A("shipu", 0, 14), A("shipi", 0, 14))
    cp(A("csend", 0, K), IND(A("colw", 0, R), A("shipu", 0, 14)))
    send("csend", 0, "colw", R, H, "acol")
    arrive([A("colw", R, PL)], "acol", INC)
    sc(A("colh", 0, R), A("colw", 0, R), 1.0, -COFF)
    tr(A("ot", 0, R), A("colh", 0, R))
    swap(7, 0, "ot", 3, 12)
    for t in range(3):
        swap(3, 24 * t, "ot", t, 12)
    tr(A("ot", R, 2 * R), A("colh", 0, R))
    tr(A("ot", 2 * R, 3 * R), A("colh", 0, R))
    for j, lane in enumerate((4, 5, 6, 7, 8, 9, 3)):
        swap(2, 72 * j, "ot", lane, 36)
    for t in range(3):
        sc(A("tn", 24 * t, 24 * t + 24), PS(7, 0, 24), 1.0 / (NR * KEY), (COFF - rank) / NR + t * R)
    tt(A("kk", 0, 144, 2), PS(3, 0, 72), A("spoti", 0, 72), OP.add)
    tt(A("kk", 1, 144, 2), PS(3, 0, 72), A("tn", 0, 72), OP.add)
    tt(A("net", 0, 48), A("kk", 0, 48), A("kk", 48, 96), OP.min)
    tt(A("net", 48, 96), A("kk", 0, 48), A("kk", 48, 96), OP.max)
    tt(A("ki", 96, 144), A("net", 48, 96), A("kk", 96, 144), OP.max)
    tt(A("net", 96, 144), A("net", 48, 96), A("kk", 96, 144), OP.min)
    dma("y", A("vb", 0, 4 * R), (T.val[:, 0:4 * R], []), ("llow", 16), after=[len(ops) - 1])
    tt(A("ki", 48, 96), A("net", 0, 48), A("net", 96, 144), OP.min)
    tt(A("ki", 0, 48), A("net", 0, 48), A("net", 96, 144), OP.max)
    ts(A("kp", 0, 144), A("ki", 0, 144), KEY - 1, OP.bitwise_and)
    ts(A("kc", 0, 72), A("ki", 0, 144, 2), 11, OP.arith_shift_right)
    cp(A("spu", 0, 72), A("kp", 0, 144, 2))
    cp(A("o3", 0, 504), PS(2, 0, 504))
    for b in range(NB):
        for w in range(B):
            s = 4 + b * B + w
            sc(A("s0", b * B * K + w, (b + 1) * B * K, B), IND(A("vb", s * R, s * R + R), A("shipu", 0, 14)))

    def own(w):
        gsel(A("u0", base[w // B] + w % B, base[w // B] + R * B, B), A("vb", (4 + w) * R, (5 + w) * R), [[0, R]], 0, 0)
    for w in range(3):
        own(w)
    for b in range(NB):
        send("s0", b * B * K, "u0", base[b] + R * B, H * B, "au0")
    arrive([A("u0", base[b] + R * B, base[b] + PL * B) for b in range(NB)], "au0", INC * NB)
    for w in range(3, 6):
        own(w)

    def xb(k):
        return (k % 2) * 1024 + 128

    def rship(k):
        sc(A("rs", (k - 1) * K, k * K), IND(A("rt%d" % k, 0, R), A("shipu", 0, 14)))
        send("rs", (k - 1) * K, "rt%d" % k, R, H, "ar%d" % k)
        arrive([A("rt%d" % k, R, PL)], "ar%d" % k, INC)

    def places(t):
        return IND(A("colw", 0, PL), A("spu", 24 * t, 24 * t + 24))
    ts(A("cg", 0, R), places(0), float(-COFF), OP.add)
    for t in (1, 2):
        sc(A("cg", t * R, t * R + R), places(t), 1.0, -COFF)
    sc(A("ext", 0, 72), PS(3, 0, 72))
    sc(A("ext", 72, 120), PS(3, 0, 48))
    cp(A("pru", 0, 72), A("kp", 1, 144, 2))
    for t in range(3):
        ts(A("low", 24 * t, 24 * t + 24), A("kc", 48 * (t > 0), 48 * (t > 0) + 24), 1.0, OP.mult)
        tr(A("ct", t * R + R, t * R + 2 * R), A("cg", t * R, t * R + R))
    for j in range(3):
        ts(A("nsp", 72 * j, 72 * j + 72), A("kp", 0, 144, 2), float(-PL), OP.add)
    sc(A("ct", 0, R), A("ct", 2 * R, 3 * R))
    sc(A("nsp", 216, 240), A("kp", 48, 96, 2), 1.0, -PL)
    sc(A("nsp", 240, 288), A("kp", 0, 96, 2), 1.0, -PL)
    sc(A("asr", 0, 3 * R), IND(A("vb", 0, 3 * R), A("pru", 0, 72)))
    for w in range(5, -1, -1):
        swap(0, 296 + 72 * w, "ct", 4 + w, 36, R)
    tt(A("ga", 0, 72), A("ext", 0, 72), A("ext", 24, 96), OP.is_gt)
    tt(A("ga", 72, 144), A("ext", 0, 72), A("ext", 48, 120), OP.is_gt)
    for bank, lo, hi in ((4, 0, 144), (5, 0, 216), (6, 72, 288)):
        mm(PS(bank, 0, hi - lo), WB, A("nsp", lo, hi), True, False)
    for w in range(6):
        mm(PS(2, 72 * w, 72 * w + 72), NKEY, A("low", 0, 72), True, False)
        swap(2, 72 * w, "ct", 4 + w, 36, 0, True)
    fn(PS(2, 0, 432), PS(2, 0, 432), AF.Abs, 1.0, 0.0)
    fn(A("eq", 42 * 72, 48 * 72), PS(2, 0, 432), AF.Relu, -1.0, 1.0)

    def weigh(sg, w, e, stop):
        c = (sg + 1) % 3 * 72 - 72 * (sg < 2)
        for v in parts[w]:
            mm(PS(4 + (sg + 1) // 3, c, c + 72), wat[v], A("eq", e, e + 72), False, stop)

    def lists(j):
        sc(A("off", max(216 * j - 72, 0), 216 * j + 144), PS(4 + j, 0, 216 if j else 144))

    def later(_):
        for t in range(3):
            sc(A("ivu", 24 * t, 24 * t + 24), PS(3, 400 + 24 * t, 424 + 24 * t), 1.0, (2 - t) * R)
        sc(A("spu", 72, 96), A("kp", 0, 48, 2))
    e0 = 0
    for d in range(-5, 7):
        w0, w1 = max(0, -d), min(5, 6 - d)
        n = (w1 - w0 + 1) * 72
        tt(A("eq", e0, e0 + n), A("o3", (d + w0) * 72, (d + w0) * 72 + n), PS(0, 296 + w0 * 72, 296 + w0 * 72 + n),
           OP.is_equal)
        for w in range(w1, w0 - 1, -1):
            weigh(d + w, w, e0 + (w - w0) * 72, w == 0 and d in (1, 4, 6))
        if d == -1:
            mm(PS(3, 400, 472), ADD, A("tn", 0, 72), True, False)
            mm(PS(3, 400, 472), WR, A("ga", 0, 72), False, False)
            mm(PS(3, 400, 472), WR, A("ga", 72, 144), False, True)
        if d == 1:
            lists(0)
            sc(A("gg", R, 3 * R), IND(A("u0", 0, TL), A("off", 48, 96)))
        if d == 4:
            for w in range(6):
                weigh(7, w, (42 + w) * 72, False)
        e0 += n
    mm(A("ps", xb(1), xb(1) + R), NID, A("asr", 2 * R, 3 * R), True, True)
    mm(A("ps", xb(1) + R, xb(1) + 2 * R), NID, A("asr", 0, R), True, True)
    nst = [0]

    def store(lo, hi):
        nst[0] += 16
        dma("y", (T.y[:, lo:hi], []), A("yb", lo, hi), ("st", 1 << 20))

    def sweep(k):
        tin = A("u%d" % (k - 1), 0, TL)
        x0 = A("asr", R, 2 * R) if k <= 2 else A("x0", 0, R)
        xo, xn = xb(k), xb(k + 1)

        def at(s):
            if s >= 7:
                return xn + (s - 7) * R
            pair = {0: 0 if k < 4 else 4, 1: 6, 2: 4 if k < 4 else 0, 3: 6}[s // 2]
            return (pair * 512 + 128 if pair else xn) + s % 2 * R

        def acc(s):
            return A("ps", at(s), at(s) + R)

        def val(s):
            c = (4 + s if s < 6 else 3) * R
            return A("vb", c, c + R) if s < 7 else A("asr", (16 - 2 * s) * R, (17 - 2 * s) * R)

        words = ORDER[k].split()
        opened = [int(x[1:]) for x in words if x[0] == "o"]
        added = [int(x[1:]) for x in words if x[0] == "b"]
        fused = [int(x[1:]) for x in words if x[0] == "f"]
        direct = [j for j in range(15) if j // 2 in opened and j % 4 in (1, 2)]
        left = {s: 1 + sum(j // 2 == s for j in added) for s in range(9)}
        flip = k == 1

        def pr(n, j, m=1):
            return A(n, j * R, (j + m) * R)

        def G(j, m):
            c = 72 * (j // 2) + 48 * (j % 2) + 24 * (j == 14)
            sc(pr("gg", j, m), IND(tin, A("off", c, c + 24 * m)))

        def Z(s):
            c = 72 * s + 24 if s < 7 else 552 if s == 7 else 504
            tt(pr("pz", s), IND(tin, A("off", c, c + 24)), x0, OP.mult)

        def M(j, m):
            c = xo + (1 - j % 2) * R
            o = A("ps", at(j // 2), at(j // 2) + m * R) if j in direct else pr("pp", j, m)
            tt(o, pr("gg", j, m), A("ps", c, c + m * R), OP.mult)

        def F(j):
            c = 72 * (j // 2) + 48 * (j % 2)
            tt(pr("pp", j), IND(tin, A("off", c, c + 24)), pr("asr", 2 * (j % 2)) if flip else pr("x1", 0), OP.mult)

        def KEEP(_):
            sc(A("x1", 0, R), acc(8))

        def OPEN(s):
            mm(acc(s), IDN, val(s), True, False)

        def SUM(s):
            left[s] -= 1
            low = flip and s == 8
            mm(acc(s), NID if low else IDN, val(s), s not in opened, False)
            mm(acc(s), ADD if low else SUB, pr("pz", s), False, left[s] == 0)

        def MORE(j):
            left[j // 2] -= 1
            mm(acc(j // 2), SUB if flip and j in fused else ADD, pr("pp", j), False, left[j // 2] == 0)

        def out(s):
            return pr("yb", 4 + s if s < 6 else 3)

        def E(s):
            rest = [j for j in (2 * s, 2 * s + 1) if j not in direct and j not in added]
            if rest:
                tt(out(s), acc(s), pr("pp", rest[0]), OP.subtract if flip and rest[0] in fused else OP.add)
            else:
                sc(out(s), acc(s))
            if k == 4:
                store((4 + s if s < 6 else 3) * R, (5 + s if s < 6 else 4) * R)

        def HALVES(s):
            for lo in (0, R // 2):
                c, p = (4 + s) * R + lo, (2 * s + (s in opened)) * R + lo
                tt(A("yb", c, c + R // 2), A("ps", at(s) + lo, at(s) + lo + R // 2), A("pp", p, p + R // 2), OP.add)
                store(c, c + R // 2)

        def C(s):
            gsel(A("u%d" % k, base[s // B] + s % B, base[s // B] + R * B, B), out(s), [[0, R]], 0, 0)

        def S(s):
            b, w = s // B, s % B
            sc(A("s%d" % k, b * B * K + w, (b + 1) * B * K, B), IND(out(s), A("shipu", 0, 14)))
            if w == B - 1:
                send("s%d" % k, b * B * K, "u%d" % k, base[b] + R * B, H * B, "au%d" % k)
            if s == 5:
                arrive([A("u%d" % k, c + R * B, c + PL * B) for c in base], "au%d" % k, INC * NB)

        def X(_):
            tt(A("x0", 0, R) if k < 4 else A("d4", 2 * R, 3 * R),
               IND(A("rt%d" % (k - 1), 0, PL), A("spu", 24, 48)), A("asr", R, 2 * R), OP.mult)

        def Q(_):
            sc(A("rr", 0, 2 * R), IND(A("rt%d" % (k - 1), 0, PL), A("spu", 48, 96)), -1.0 if k < 4 else 1.0)

        def L(_):
            if flip:
                return sc(acc(7), acc(7), -1.0)
            tt(A("ps", xn, xn + 2 * R) if k < 4 else A("d4", 0, 2 * R), A("ps", xn, xn + 2 * R), A("rr", 0, 2 * R), OP.mult)

        def Y(_):
            sc(A("yb", 0, 3 * R), IND(A("d4", 0, 3 * R), A("ivu", 0, 72)))
            store(0, 3 * R)

        def RN(j):
            rk = A("rt%d" % k, 0, R)
            if j == 0:
                tt(acc(6), acc(6), rk, OP.mult)
            elif j == 1:
                sc(acc(6), acc(6), -1.0, 2.0)
            else:
                tt(A("rt%d" % (k + 1), 0, R), acc(6), rk, OP.mult)
                if k == 3:
                    nst[0] += 16
                    dma("y", (T.inv[:], []), A("rt4", 0, R), ("st", 1 << 20))

        def W(_):
            if k == 1:
                sc(A("rt1", 0, R), A("vb", 3 * R, 4 * R), -1.0, 2.0)
            rship(k)

        return {"g": lambda j: G(j, 1), "G": lambda j: G(j, 2), "m": lambda j: M(j, 1), "M": lambda j: M(j, 2),
                "z": Z, "o": OPEN, "a": SUM, "b": MORE, "e": E, "c": C, "s": S, "x": X, "q": Q, "l": L, "y": Y,
                "r": RN, "w": W, "f": F, "k": KEEP, "d": lists, "i": later, "h": HALVES}

    steps = {k: sweep(k) for k in range(1, 5)}
    for k in range(1, 5):
        for word in ORDER[k].split():
            back = word[0] == "<"
            steps[k - back][word[back]](int(word[back + 1:] or 0))
    _emit(g, T, ops, [("g", "sent", nsent[0]), ("y", "st", nst[0])])
